import numpy as np
import ml_dtypes


def mxq(x, axis, fmt="e4m3"):
    dtype, down = {"e4m3": (ml_dtypes.float8_e4m3fn, 7), "e5m2": (ml_dtypes.float8_e5m2, 14)}[fmt]
    v = np.moveaxis(np.asarray(x, np.float32).astype(ml_dtypes.bfloat16).astype(np.float64), axis, -1)
    blocks = v.reshape(v.shape[:-1] + (-1, 32))
    amax = np.abs(blocks).max(-1, keepdims=True)
    byte = np.maximum(np.where(amax > 0, np.frexp(amax)[1] - 1 + 127, 0) - down, 1)
    scale = np.exp2(byte - 127.0)
    codes = (blocks / scale).astype(np.float32).astype(dtype).astype(np.float64)
    return np.moveaxis((codes * scale).reshape(v.shape), -1, axis)


WIDE = False


def mx_kscale(k):
    if not WIDE:
        return np.ones(k)
    levels = np.array([10, -10, 5, -5, 0])
    if k % 512:
        return np.exp2(np.random.permutation(np.resize(levels, k // 32))).repeat(32)
    a = np.empty((k // 512, 16))
    for p in range(k // 512):
        a[p, :8] = np.random.permutation(np.resize(levels, 8))
        for g in range(8):
            far = levels[np.abs(levels - a[p, g]) >= 10]
            a[p, g + 8] = far[np.random.randint(len(far))]
    return np.exp2(a.ravel()).repeat(32)


def f64(x):
    return np.asarray(x).astype(np.float64)


def striped(idx):
    return np.tile(np.asarray(idx).reshape(-1, 16).T, (8, 1)).astype(np.uint16)


def unstriped(offs):
    return offs[:16].T.reshape(-1).astype(np.int64)


E2M1 = np.array([0.0, 0.5, 1.0, 1.5, 2.0, 3.0, 4.0, 6.0, -0.0, -0.5, -1.0, -1.5, -2.0, -3.0, -4.0, -6.0])


def pack_weight(w, fmt):
    k, n = w.shape
    w = f64(np.asarray(w, np.float32).astype(ml_dtypes.bfloat16)).reshape(k // 32, 32, n)
    amax = np.abs(w).max(1)
    if fmt == "e4m3":
        byte = np.frexp(amax)[1] - 1 + 127 - 7
    else:
        mant, ex = np.frexp(amax / 6.0)
        byte = np.where(mant > 0.5, ex, ex - 1) + 127
    byte = np.clip(np.where(amax > 0, byte, 1), 1, 254)
    scaled = (w * np.exp2(127.0 - byte)[:, None, :]).reshape(k, n).astype(np.float32)
    by_word = np.ascontiguousarray(scaled.reshape(k // 512, 128, 4, n).transpose(0, 1, 3, 2))
    if fmt == "e4m3":
        words = by_word.astype(ml_dtypes.float8_e4m3fn).view(np.uint8)
    else:
        c = by_word.astype(ml_dtypes.float4_e2m1fn).view(np.uint8) & 0xF
        words = (c[..., 0::2] | (c[..., 1::2] << 4)).reshape(k // 512, 128, 2 * n)
    return np.ascontiguousarray(words), np.ascontiguousarray(byte.astype(np.uint8).reshape(k // 512, 16, n))


def unpack_weight(words, scales, fmt):
    g, _, n = scales.shape
    words = np.ascontiguousarray(words).reshape(g, 128, n, -1)
    if fmt == "e4m3":
        vals = words.view(ml_dtypes.float8_e4m3fn).astype(np.float64)
    else:
        nib = np.empty((g, 128, n, 4), np.uint8)
        nib[..., 0::2] = words & 0xF
        nib[..., 1::2] = words >> 4
        vals = E2M1[nib]
    vals = vals * np.repeat(np.exp2(scales.astype(np.float64) - 127.0), 8, axis=1)[..., None]
    return vals.transpose(0, 1, 3, 2).reshape(g * 512, n)


def softplus(v):
    return np.log(1.0 + np.exp(v))


def sigmoid(v):
    return 1.0 / (1.0 + np.exp(-v))


D, K, R, T, I, Q = 512, 512, 512, 2048, 512, 128


def setup_inputs():
    n = np.random.standard_normal
    idx3 = np.random.permutation(I)[:I]
    idx = np.random.permutation(T)[:I]
    fd = mx_kscale(D)
    fk = mx_kscale(K)
    fr = mx_kscale(R)
    keysp = pack_weight(n((D, T)) / fd[:, None], "e4m3")
    tabp = pack_weight(n((K, T)) / fk[:, None], "e4m3")
    return {
        "query": (n((D, Q)) * 0.9 / np.sqrt(D) * fd[:, None]).astype(np.float32),
        "keys_words": keysp[0],
        "keys_scales": keysp[1],
        "th": (np.random.uniform(-0.3, 0.6, (Q, 1))).astype(np.float32),
        "reserve": (np.random.uniform(50.0, 200.0, (Q, 1))).astype(np.float32),
        "tab_words": tabp[0],
        "tab_scales": tabp[1],
        "w1": (n((K, R)) * 1 / np.sqrt(K) * fk[:, None]).astype(np.float32),
        "lam": (np.random.uniform(0.3, 1.0, (R, 1))).astype(np.float32),
        "gout": (n((R, Q)) * 1 / np.sqrt(R) * fr[:, None]).astype(np.float32),
        "hsc": (np.random.uniform(0.7, 1.4, (R, 1)) / fr[:, None]).astype(np.float32),
        "old": (0.5 * n((Q, T))).astype(np.float32),
        "offs3": striped(idx3),
        "offs": striped(idx),
    }


def reference(query, keys_words, keys_scales, th, reserve, tab_words, tab_scales, w1, lam, gout, hsc, old, offs3, offs):
    idx3 = unstriped(offs3)
    idx = unstriped(offs)
    keysu = unpack_weight(keys_words, keys_scales, "e4m3")
    tabu = unpack_weight(tab_words, tab_scales, "e4m3")
    queryq = mxq(f64(query), 0, "e4m3")
    keysidxg = keysu[:, idx]
    a = queryq.T @ keysidxg
    p = softplus(a - f64(th))
    z = np.sum(p, axis=1, keepdims=True) + f64(reserve)
    w1q = mxq(f64(w1), 0, "e4m3")
    tabidxg = tabu[:, idx]
    zh = w1q.T @ tabidxg
    ht = softplus(zh)
    hv = ht + ht[:, idx3] * f64(lam)
    hs1 = hv * f64(hsc)
    goutq = mxq(f64(gout), 0, "e4m3")
    hs1q = mxq(hs1, 0, "e4m3")
    c0 = goutq.T @ hs1q
    dz = np.sum(c0 * p / np.square(z) * (-1.0), axis=1, keepdims=True)
    dp = c0 / z + dz
    da = dp * sigmoid(a - f64(th))
    gs = da * 512.0
    gf = np.zeros((Q, T))
    gf[:, idx] = gs
    y = f64(old) + gf
    return y

@@ -1,0 +1,268 @@
+from contextlib import ExitStack
+
+import concourse.mybir as mybir
+
+F32 = mybir.dt.float32
+BF16 = mybir.dt.bfloat16
+I32 = mybir.dt.int32
+U32 = mybir.dt.uint32
+U16 = mybir.dt.uint16
+U8 = mybir.dt.uint8
+FP8X4 = mybir.dt.float8_e4m3fn_x4
+ALU = mybir.AluOpType
+ACT = mybir.ActivationFunctionType
+
+P = 128
+PACK = 4
+T = 2048
+SLOTS = 512
+HALF = SLOTS // 2
+SPARE = 192
+CAP = 41.5
+W1_SPLIT = 96
+OUT_CHUNK = 512
+
+FLOPS = 2 * 512 * 512 * (128 + 512 + 128)
+
+
+def tile_attend_blrlent_capped_kernel(
+    tc, query, keys_words, keys_scales, th, reserve, tab_words, tab_scales, w1, lam, gout, hsc, old, offs3, offs, out
+):
+    nc = tc.nc
+    with ExitStack() as ctx:
+        lists = ctx.enter_context(tc.tile_pool(name="lists", bufs=1))
+        sb = ctx.enter_context(tc.tile_pool(name="sb", bufs=1))
+        ps = ctx.enter_context(tc.psum_pool(name="ps", bufs=1))
+
+        def load_scale_rows(queue, plane, scales):
+            for quad in range(4):
+                queue.dma_start(
+                    out=plane[32 * quad : 32 * quad + 4, :].bitcast(I32),
+                    in_=scales[0, 4 * quad : 4 * quad + 4, :].bitcast(I32),
+                )
+
+        def load_words(pool_tile, words):
+            nc.sync.dma_start(
+                out=pool_tile[:].bitcast(I32), in_=words[0].rearrange("p n t -> p (n t)").bitcast(I32)
+            )
+
+        tab_plane = sb.tile([P, T], U8, name="tab_plane", tag="small_a", align_bytes=64)
+        nc.vector.memset(tab_plane[:].bitcast(I32), 0)
+        neg_cap = sb.tile([P, 1], F32, name="neg_cap", tag="big_b", align_bytes=64)
+        nc.vector.memset(neg_cap[:], -CAP)
+        key_plane = sb.tile([P, T], U8, name="key_plane", align_bytes=64)
+        nc.gpsimd.memset(key_plane[:].bitcast(I32), 0)
+        ht = [sb.tile([P, SLOTS + SPARE], F32, name=f"ht{j}") for j in range(PACK)]
+        for j in range(PACK):
+            nc.vector.memset(ht[j][:, SLOTS:], 0.0)
+        placed = sb.tile([P, T], F32, name="placed")
+        nc.vector.memset(placed[:], 0.0)
+        tiny = sb.tile([P, 1], F32, name="tiny")
+        nc.scalar.activation(tiny[:], neg_cap[:], ACT.Sigmoid)
+
+        idx = lists.tile([P, SLOTS // 16], U16, name="idx")
+        nc.sync.dma_start(idx[:], offs)
+        w1_raw = sb.tile([P, PACK, 512], F32, name="w1_raw", tag="big_a")
+        nc.sync.dma_start(out=w1_raw[:], in_=w1.rearrange("(p t) r -> p t r", t=PACK))
+        load_scale_rows(nc.sync, tab_plane, tab_scales)
+        tab_pool = sb.tile([P, T], U32, name="tab_pool", tag="big_b", align_bytes=64)
+        load_words(tab_pool, tab_words)
+        link = lists.tile([P, SLOTS // 16], U16, name="link")
+        nc.sync.dma_start(link[:], offs3)
+
+        load_scale_rows(nc.gpsimd, key_plane, keys_scales)
+        lam_sb = sb.tile([P, PACK], F32, name="lam_sb")
+        nc.gpsimd.dma_start(out=lam_sb[:], in_=lam.rearrange("(p j) o -> p (j o)", j=PACK))
+        hsc_sb = sb.tile([P, PACK], F32, name="hsc_sb")
+        nc.gpsimd.dma_start(out=hsc_sb[:], in_=hsc.rearrange("(p j) o -> p (j o)", j=PACK))
+        th_sb = sb.tile([P, 1], F32, name="th_sb")
+        nc.gpsimd.dma_start(out=th_sb[:], in_=th)
+        reserve_sb = sb.tile([P, 1], F32, name="reserve_sb")
+        nc.gpsimd.dma_start(out=reserve_sb[:], in_=reserve)
+
+        tab_bytes = sb.tile([P, SLOTS], U8, name="tab_bytes", align_bytes=64)
+        nc.vector.tensor_copy(tab_bytes[:], tab_plane[:].indirect(idx[:]))
+        w1_bf = sb.tile([P, PACK, P, PACK], BF16, name="w1_bf", align_bytes=64)
+        w1_dst = w1_bf[:].rearrange("p j m t -> p m t j")
+        w1_src = w1_raw[:].rearrange("p t (m j) -> p m t j", j=PACK)
+        nc.scalar.copy(w1_dst[:, :W1_SPLIT], w1_src[:, :W1_SPLIT])
+        nc.vector.tensor_copy(w1_dst[:, W1_SPLIT:], w1_src[:, W1_SPLIT:])
+        w1_codes = sb.tile([P, 512], U32, name="w1_codes", align_bytes=64)
+        w1_bytes = sb.tile([P, 512], U8, name="w1_bytes", align_bytes=64)
+        nc.vector.quantize_mx(
+            out=w1_codes[:].bitcast(FP8X4), scales=w1_bytes[:], in_=w1_bf[:].rearrange("p j m t -> p (j m t)")
+        )
+        tab_codes = sb.tile([P, SLOTS], U32, name="tab_codes", align_bytes=64)
+        nc.vector.tensor_copy(tab_codes[:], tab_pool[:].indirect(idx[:]))
+
+        q_raw = sb.tile([P, PACK, P], F32, name="q_raw", tag="small_a", align_bytes=64)
+        nc.sync.dma_start(out=q_raw[:], in_=query.rearrange("(p t) q -> p t q", t=PACK))
+        key_pool = sb.tile([P, T], U32, name="key_pool", tag="big_a")
+        load_words(key_pool, keys_words)
+
+        zh = [ps.tile([P, SLOTS], F32, name=f"zh{j}") for j in range(PACK)]
+        for j in range(PACK):
+            cols = slice(j * P, (j + 1) * P)
+            nc.tensor.matmul_mx(
+                out=zh[j][:],
+                lhsT=w1_codes[:, cols].bitcast(FP8X4),
+                lhsT_scale=w1_bytes[:, cols],
+                rhs=tab_codes[:].bitcast(FP8X4),
+                rhs_scale=tab_bytes[:],
+                start=True,
+                stop=True,
+            )
+        sig_neg = [sb.tile([P, SLOTS], F32, name=f"sig_neg{j}") for j in range(PACK)]
+        for j in range(PACK):
+            nc.scalar.activation(sig_neg[j][:], zh[j][:], ACT.Sigmoid, scale=-1.0)
+
+        q_bf = sb.tile([P, P, PACK], BF16, name="q_bf", align_bytes=64)
+        key_bytes = sb.tile([P, SLOTS], U8, name="key_bytes", tag="big_b", align_bytes=64)
+        nc.vector.tensor_scalar(
+            q_bf[:].rearrange("p (c i) t -> p c t i", i=4),
+            q_raw[:].rearrange("p t (c i) -> p c t i", i=4),
+            -1.0,
+            None,
+            ALU.mult,
+        )
+        nc.vector.tensor_copy(key_bytes[:], key_plane[:].indirect(idx[:]))
+        q_codes = sb.tile([P, P], U32, name="q_codes", align_bytes=64)
+        q_bytes = sb.tile([P, P], U8, name="q_bytes", align_bytes=64)
+        nc.vector.quantize_mx(
+            out=q_codes[:].bitcast(FP8X4), scales=q_bytes[:], in_=q_bf[:].rearrange("p q t -> p (q t)")
+        )
+        key_codes = sb.tile([P, SLOTS], U32, name="key_codes", align_bytes=64)
+        nc.vector.tensor_copy(key_codes[:], key_pool[:].indirect(idx[:]))
+        neg_a = ps.tile([P, SLOTS], F32, name="neg_a")
+        nc.tensor.matmul_mx(
+            out=neg_a[:],
+            lhsT=q_codes[:].bitcast(FP8X4),
+            lhsT_scale=q_bytes[:],
+            rhs=key_codes[:].bitcast(FP8X4),
+            rhs_scale=key_bytes[:],
+            start=True,
+            stop=True,
+        )
+        neg_th = sb.tile([P, 1], F32, name="neg_th")
+        nc.gpsimd.tensor_scalar(neg_th[:], th_sb[:], -1.0, 0.0, ALU.mult, ALU.add)
+
+        lam_hsc = sb.tile([P, PACK], F32, name="lam_hsc")
+        nc.gpsimd.tensor_tensor(lam_hsc[:], lam_sb[:], hsc_sb[:], ALU.mult)
+
+        g_raw = sb.tile([P, PACK, P], F32, name="g_raw", tag="small_a", align_bytes=64)
+        nc.sync.dma_start(out=g_raw[:], in_=gout.rearrange("(p t) q -> p t q", t=PACK))
+        old_sb = sb.tile([P, T], F32, name="old_sb", tag="big_a")
+        nc.sync.dma_start(out=old_sb[:], in_=old)
+
+        g_bf = sb.tile([P, P, PACK], BF16, name="g_bf", align_bytes=64)
+        nc.vector.tensor_copy(
+            g_bf[:].rearrange("p (c i) t -> p c t i", i=4), g_raw[:].rearrange("p t (c i) -> p c t i", i=4)
+        )
+        g_codes = sb.tile([P, P], U32, name="g_codes", align_bytes=64)
+        g_bytes = sb.tile([P, P], U8, name="g_bytes", align_bytes=64)
+        nc.vector.quantize_mx(
+            out=g_codes[:].bitcast(FP8X4), scales=g_bytes[:], in_=g_bf[:].rearrange("p q t -> p (q t)")
+        )
+
+        log_sig = [sb.tile([P, SLOTS], F32, name=f"log_sig{j}") for j in range(PACK)]
+        for j in range(PACK):
+            nc.scalar.activation(log_sig[j][:], sig_neg[j][:], ACT.Ln, bias=tiny[:])
+
+        linked = [sb.tile([P, SLOTS], F32, name=f"linked{j}") for j in range(PACK)]
+        own = [sb.tile([P, SLOTS], F32, name=f"own{j}") for j in range(PACK)]
+        hs_planes = sb.tile([P, PACK, SLOTS], BF16, name="hs_planes")
+
+        def finish_softplus(j):
+            nc.vector.scalar_tensor_tensor(ht[j][:, :SLOTS], log_sig[j][:], -1.0, zh[j][:], ALU.mult, ALU.max)
+            nc.scalar.activation(own[j][:], ht[j][:, :SLOTS], ACT.Copy, scale=hsc_sb[:, j : j + 1])
+
+        def look_up(j):
+            nc.vector.tensor_copy(linked[j][:], ht[j][:].indirect(link[:]))
+
+        def combine(j):
+            nc.vector.scalar_tensor_tensor(
+                hs_planes[:, j, :], linked[j][:], lam_hsc[:, j : j + 1], own[j][:], ALU.mult, ALU.add
+            )
+
+        finish_softplus(0)
+        finish_softplus(1)
+        look_up(0)
+        finish_softplus(2)
+        finish_softplus(3)
+        sig_neg_a = sb.tile([P, SLOTS], F32, name="sig_neg_a")
+        nc.scalar.activation(sig_neg_a[:], neg_a[:], ACT.Sigmoid, bias=th_sb[:])
+        sig_a = sb.tile([P, SLOTS], F32, name="sig_a")
+        nc.scalar.activation(sig_a[:], neg_a[:], ACT.Sigmoid, bias=neg_th[:], scale=-1.0)
+        log_sig_a = sb.tile([P, SLOTS], F32, name="log_sig_a")
+        nc.scalar.activation(log_sig_a[:], sig_neg_a[:], ACT.Ln, bias=tiny[:])
+        look_up(1)
+        combine(0)
+        look_up(2)
+        combine(1)
+        look_up(3)
+        combine(2)
+
+        combine(3)
+        neg_p = sb.tile([P, SLOTS], F32, name="neg_p")
+        neg_sum = sb.tile([P, 1], F32, name="neg_sum")
+        nc.vector.scalar_tensor_tensor(
+            neg_p[:], neg_a[:], th_sb[:], log_sig_a[:], ALU.add, ALU.min, accum_out=neg_sum[:]
+        )
+        z = sb.tile([P, 1], F32, name="z")
+        nc.vector.tensor_scalar(z[:], neg_sum[:], -1.0, reserve_sb[:], ALU.mult, ALU.add)
+
+        hs_bf = sb.tile([P, SLOTS, PACK], BF16, name="hs_bf", align_bytes=64)
+        hs_codes = sb.tile([P, SLOTS], U32, name="hs_codes", align_bytes=64)
+        hs_bytes = sb.tile([P, SLOTS], U8, name="hs_bytes", align_bytes=64)
+        c0 = ps.tile([P, SLOTS], F32, name="c0")
+
+        def scale_and_weave(h):
+            cols = slice(h * HALF, (h + 1) * HALF)
+            nc.vector.tensor_copy(
+                hs_bf[:, cols, :].rearrange("p (c i) t -> p c t i", i=4),
+                hs_planes[:, :, cols].rearrange("p t (c i) -> p c t i", i=4),
+            )
+
+        def quantise_and_multiply(h):
+            cols = slice(h * HALF, (h + 1) * HALF)
+            nc.vector.quantize_mx(
+                out=hs_codes[:, cols].bitcast(FP8X4),
+                scales=hs_bytes[:, cols],
+                in_=hs_bf[:, cols, :].rearrange("p i t -> p (i t)"),
+            )
+            nc.tensor.matmul_mx(
+                out=c0[:, cols],
+                lhsT=g_codes[:].bitcast(FP8X4),
+                lhsT_scale=g_bytes[:],
+                rhs=hs_codes[:, cols].bitcast(FP8X4),
+                rhs_scale=hs_bytes[:, cols],
+                start=True,
+                stop=True,
+            )
+
+        scale_and_weave(0)
+        inv_z = sb.tile([P, 1], F32, name="inv_z")
+        nc.vector.reciprocal(inv_z[:], z[:])
+        scale_and_weave(1)
+        quantise_and_multiply(0)
+        gain = sb.tile([P, 1], F32, name="gain")
+        nc.vector.tensor_scalar(gain[:], inv_z[:], 512.0, None, ALU.mult)
+        gain_sq = sb.tile([P, 1], F32, name="gain_sq")
+        nc.vector.tensor_scalar(gain_sq[:], inv_z[:], inv_z[:], 512.0, ALU.mult, ALU.mult)
+        quantise_and_multiply(1)
+
+        terms = sb.tile([P, SLOTS], F32, name="terms")
+        dz = sb.tile([P, 1], F32, name="dz")
+        nc.vector.scalar_tensor_tensor(
+            terms[:], c0[:], gain_sq[:], neg_p[:], ALU.mult, ALU.mult, accum_out=dz[:]
+        )
+        dp = sb.tile([P, SLOTS], F32, name="dp")
+        nc.vector.tensor_scalar(dp[:], c0[:], gain[:], dz[:], ALU.mult, ALU.add)
+        nc.vector.tensor_tensor(placed[:].indirect(idx[:]), dp[:], sig_a[:], ALU.mult)
+
+        for n in range(T // OUT_CHUNK):
+            cols = slice(n * OUT_CHUNK, (n + 1) * OUT_CHUNK)
+            total = sb.tile([P, OUT_CHUNK], F32, name=f"total{n}")
+            nc.vector.tensor_tensor(total[:], placed[:, cols], old_sb[:, cols], ALU.add)
+            queue = nc.sync if n % 2 == 0 else nc.scalar
+            queue.dma_start(out=out[:, cols], in_=total[:])

@@ -19,10 +19,24 @@ SLOTS = 512
 HALF = SLOTS // 2
 SPARE = 192
 CAP = 41.5
-W1_SPLIT = 96
+W1_SPLIT = 84
 OUT_CHUNK = 512
+TAB_AT, KEY_AT, PLANE_AT = 0, 4 * T, 8 * T
+Q_AT = PLANE_AT + T
+G_AT = Q_AT + 1024
+W1_AT = G_AT + 1024
+HT_COLS = PACK * SLOTS + SPARE
+HT_AT = W1_AT - 4 * HT_COLS
 
 FLOPS = 2 * 512 * 512 * (128 + 512 + 128)
+
+
+def half(h):
+    return slice(h * HALF, (h + 1) * HALF)
+
+
+def half_list(h):
+    return slice(h * HALF // 16, (h + 1) * HALF // 16)
 
 
 def tile_attend_blrlent_capped_kernel(
@@ -32,6 +46,7 @@ def tile_attend_blrlent_capped_kernel(
     with ExitStack() as ctx:
         lists = ctx.enter_context(tc.tile_pool(name="lists", bufs=1))
         sb = ctx.enter_context(tc.tile_pool(name="sb", bufs=1))
+        shared = ctx.enter_context(tc.tile_pool(name="shared", bufs=1))
         ps = ctx.enter_context(tc.psum_pool(name="ps", bufs=1))
 
         def load_scale_rows(queue, plane, scales):
@@ -46,39 +61,29 @@ def tile_attend_blrlent_capped_kernel(
                 out=pool_tile[:].bitcast(I32), in_=words[0].rearrange("p n t -> p (n t)").bitcast(I32)
             )
 
-        tab_plane = sb.tile([P, T], U8, name="tab_plane", tag="small_a", align_bytes=64)
+        tab_plane = sb.tile([P, T], U8, name="tab_plane", tag="plane", align_bytes=64)
         nc.vector.memset(tab_plane[:].bitcast(I32), 0)
-        neg_cap = sb.tile([P, 1], F32, name="neg_cap", tag="big_b", align_bytes=64)
+        neg_cap = shared.tile([P, 16], F32, name="neg_cap", offset=KEY_AT - 32)
         nc.vector.memset(neg_cap[:], -CAP)
-        key_plane = sb.tile([P, T], U8, name="key_plane", align_bytes=64)
-        nc.gpsimd.memset(key_plane[:].bitcast(I32), 0)
-        ht = [sb.tile([P, SLOTS + SPARE], F32, name=f"ht{j}") for j in range(PACK)]
-        for j in range(PACK):
-            nc.vector.memset(ht[j][:, SLOTS:], 0.0)
         placed = sb.tile([P, T], F32, name="placed")
         nc.vector.memset(placed[:], 0.0)
+        key_plane = shared.tile([P, T], U8, name="key_plane", offset=PLANE_AT)
+        nc.vector.memset(key_plane[:].bitcast(I32), 0)
         tiny = sb.tile([P, 1], F32, name="tiny")
-        nc.scalar.activation(tiny[:], neg_cap[:], ACT.Sigmoid)
+        nc.scalar.activation(tiny[:], neg_cap[:, 0:1], ACT.Sigmoid)
 
         idx = lists.tile([P, SLOTS // 16], U16, name="idx")
         nc.sync.dma_start(idx[:], offs)
-        w1_raw = sb.tile([P, PACK, 512], F32, name="w1_raw", tag="big_a")
+        w1_raw = shared.tile([P, PACK, 512], F32, name="w1_raw", offset=W1_AT)
         nc.sync.dma_start(out=w1_raw[:], in_=w1.rearrange("(p t) r -> p t r", t=PACK))
         load_scale_rows(nc.sync, tab_plane, tab_scales)
-        tab_pool = sb.tile([P, T], U32, name="tab_pool", tag="big_b", align_bytes=64)
+        tab_pool = shared.tile([P, T], U32, name="tab_pool", offset=TAB_AT)
         load_words(tab_pool, tab_words)
         link = lists.tile([P, SLOTS // 16], U16, name="link")
         nc.sync.dma_start(link[:], offs3)
-
-        load_scale_rows(nc.gpsimd, key_plane, keys_scales)
-        lam_sb = sb.tile([P, PACK], F32, name="lam_sb")
-        nc.gpsimd.dma_start(out=lam_sb[:], in_=lam.rearrange("(p j) o -> p (j o)", j=PACK))
-        hsc_sb = sb.tile([P, PACK], F32, name="hsc_sb")
-        nc.gpsimd.dma_start(out=hsc_sb[:], in_=hsc.rearrange("(p j) o -> p (j o)", j=PACK))
-        th_sb = sb.tile([P, 1], F32, name="th_sb")
-        nc.gpsimd.dma_start(out=th_sb[:], in_=th)
-        reserve_sb = sb.tile([P, 1], F32, name="reserve_sb")
-        nc.gpsimd.dma_start(out=reserve_sb[:], in_=reserve)
+        key_pool = shared.tile([P, T], U32, name="key_pool", offset=KEY_AT)
+        load_words(key_pool, keys_words)
+        load_scale_rows(nc.sync, key_plane, keys_scales)
 
         tab_bytes = sb.tile([P, SLOTS], U8, name="tab_bytes", align_bytes=64)
         nc.vector.tensor_copy(tab_bytes[:], tab_plane[:].indirect(idx[:]))
@@ -87,37 +92,50 @@ def tile_attend_blrlent_capped_kernel(
         w1_src = w1_raw[:].rearrange("p t (m j) -> p m t j", j=PACK)
         nc.scalar.copy(w1_dst[:, :W1_SPLIT], w1_src[:, :W1_SPLIT])
         nc.vector.tensor_copy(w1_dst[:, W1_SPLIT:], w1_src[:, W1_SPLIT:])
-        w1_codes = sb.tile([P, 512], U32, name="w1_codes", align_bytes=64)
+        w1_codes = sb.tile([P, 512], U32, name="w1_codes", tag="plane", align_bytes=64)
         w1_bytes = sb.tile([P, 512], U8, name="w1_bytes", align_bytes=64)
         nc.vector.quantize_mx(
             out=w1_codes[:].bitcast(FP8X4), scales=w1_bytes[:], in_=w1_bf[:].rearrange("p j m t -> p (j m t)")
         )
         tab_codes = sb.tile([P, SLOTS], U32, name="tab_codes", align_bytes=64)
-        nc.vector.tensor_copy(tab_codes[:], tab_pool[:].indirect(idx[:]))
+        for h in range(2):
+            nc.vector.tensor_copy(tab_codes[:, half(h)], tab_pool[:].indirect(idx[:, half_list(h)]))
 
-        q_raw = sb.tile([P, PACK, P], F32, name="q_raw", tag="small_a", align_bytes=64)
+        q_raw = shared.tile([P, PACK, P], F32, name="q_raw", offset=W1_AT)
         nc.sync.dma_start(out=q_raw[:], in_=query.rearrange("(p t) q -> p t q", t=PACK))
-        key_pool = sb.tile([P, T], U32, name="key_pool", tag="big_a")
-        load_words(key_pool, keys_words)
+        g_raw = shared.tile([P, PACK, P], F32, name="g_raw", offset=W1_AT + 2048)
+        nc.sync.dma_start(out=g_raw[:], in_=gout.rearrange("(p t) q -> p t q", t=PACK))
+        lam_sb = shared.tile([P, PACK], F32, name="lam_sb", offset=W1_AT + 4096)
+        nc.sync.dma_start(out=lam_sb[:], in_=lam.rearrange("(p j) o -> p (j o)", j=PACK))
+        hsc_sb = shared.tile([P, PACK], F32, name="hsc_sb", offset=W1_AT + 4096 + 64)
+        nc.sync.dma_start(out=hsc_sb[:], in_=hsc.rearrange("(p j) o -> p (j o)", j=PACK))
+        th_sb = shared.tile([P, 1], F32, name="th_sb", offset=W1_AT + 4096 + 128)
+        nc.sync.dma_start(out=th_sb[:], in_=th)
+        reserve_sb = shared.tile([P, 1], F32, name="reserve_sb", offset=W1_AT + 4096 + 192)
+        nc.sync.dma_start(out=reserve_sb[:], in_=reserve)
 
-        zh = [ps.tile([P, SLOTS], F32, name=f"zh{j}") for j in range(PACK)]
-        for j in range(PACK):
-            cols = slice(j * P, (j + 1) * P)
-            nc.tensor.matmul_mx(
-                out=zh[j][:],
-                lhsT=w1_codes[:, cols].bitcast(FP8X4),
-                lhsT_scale=w1_bytes[:, cols],
-                rhs=tab_codes[:].bitcast(FP8X4),
-                rhs_scale=tab_bytes[:],
-                start=True,
-                stop=True,
-            )
-        sig_neg = [sb.tile([P, SLOTS], F32, name=f"sig_neg{j}") for j in range(PACK)]
-        for j in range(PACK):
-            nc.scalar.activation(sig_neg[j][:], zh[j][:], ACT.Sigmoid, scale=-1.0)
+        parts = [(g, h) for h in range(2) for g in range(2)]
+        zh = {part: ps.tile([P, 2, HALF], F32, name=f"zh{part[0]}{part[1]}") for part in parts}
+        sig_neg = {part: sb.tile([P, 2, HALF], F32, name=f"sig_neg{part[0]}{part[1]}") for part in parts}
+        for g, h in parts:
+            for e in range(2):
+                cols = slice((2 * g + e) * P, (2 * g + e + 1) * P)
+                nc.tensor.matmul_mx(
+                    out=zh[g, h][:, e, :],
+                    lhsT=w1_codes[:, cols].bitcast(FP8X4),
+                    lhsT_scale=w1_bytes[:, cols],
+                    rhs=tab_codes[:, half(h)].bitcast(FP8X4),
+                    rhs_scale=tab_bytes[:, half(h)],
+                    start=True,
+                    stop=True,
+                )
+            nc.scalar.activation(sig_neg[g, h][:], zh[g, h][:], ACT.Sigmoid, scale=-1.0)
 
-        q_bf = sb.tile([P, P, PACK], BF16, name="q_bf", align_bytes=64)
-        key_bytes = sb.tile([P, SLOTS], U8, name="key_bytes", tag="big_b", align_bytes=64)
+        q_bf = shared.tile([P, P, PACK], BF16, name="q_bf", offset=Q_AT, align_bytes=64)
+        key_bytes = sb.tile([P, SLOTS], U8, name="key_bytes", align_bytes=64)
+        key_codes = sb.tile([P, SLOTS], U32, name="key_codes", align_bytes=64)
+        nc.vector.tensor_copy(key_codes[:], key_pool[:].indirect(idx[:]))
+        nc.vector.tensor_copy(key_bytes[:], key_plane[:].indirect(idx[:]))
         nc.vector.tensor_scalar(
             q_bf[:].rearrange("p (c i) t -> p c t i", i=4),
             q_raw[:].rearrange("p t (c i) -> p c t i", i=4),
@@ -125,14 +143,15 @@ def tile_attend_blrlent_capped_kernel(
             None,
             ALU.mult,
         )
-        nc.vector.tensor_copy(key_bytes[:], key_plane[:].indirect(idx[:]))
+        g_bf = shared.tile([P, P, PACK], BF16, name="g_bf", offset=G_AT, align_bytes=64)
+        nc.vector.tensor_copy(
+            g_bf[:].rearrange("p (c i) t -> p c t i", i=4), g_raw[:].rearrange("p t (c i) -> p c t i", i=4)
+        )
         q_codes = sb.tile([P, P], U32, name="q_codes", align_bytes=64)
         q_bytes = sb.tile([P, P], U8, name="q_bytes", align_bytes=64)
         nc.vector.quantize_mx(
             out=q_codes[:].bitcast(FP8X4), scales=q_bytes[:], in_=q_bf[:].rearrange("p q t -> p (q t)")
         )
-        key_codes = sb.tile([P, SLOTS], U32, name="key_codes", align_bytes=64)
-        nc.vector.tensor_copy(key_codes[:], key_pool[:].indirect(idx[:]))
         neg_a = ps.tile([P, SLOTS], F32, name="neg_a")
         nc.tensor.matmul_mx(
             out=neg_a[:],
@@ -149,116 +168,109 @@ def tile_attend_blrlent_capped_kernel(
         lam_hsc = sb.tile([P, PACK], F32, name="lam_hsc")
         nc.gpsimd.tensor_tensor(lam_hsc[:], lam_sb[:], hsc_sb[:], ALU.mult)
 
-        g_raw = sb.tile([P, PACK, P], F32, name="g_raw", tag="small_a", align_bytes=64)
-        nc.sync.dma_start(out=g_raw[:], in_=gout.rearrange("(p t) q -> p t q", t=PACK))
-        old_sb = sb.tile([P, T], F32, name="old_sb", tag="big_a")
+        old_sb = shared.tile([P, T], F32, name="old_sb", offset=TAB_AT)
         nc.sync.dma_start(out=old_sb[:], in_=old)
 
-        g_bf = sb.tile([P, P, PACK], BF16, name="g_bf", align_bytes=64)
-        nc.vector.tensor_copy(
-            g_bf[:].rearrange("p (c i) t -> p c t i", i=4), g_raw[:].rearrange("p t (c i) -> p c t i", i=4)
-        )
         g_codes = sb.tile([P, P], U32, name="g_codes", align_bytes=64)
         g_bytes = sb.tile([P, P], U8, name="g_bytes", align_bytes=64)
         nc.vector.quantize_mx(
             out=g_codes[:].bitcast(FP8X4), scales=g_bytes[:], in_=g_bf[:].rearrange("p q t -> p (q t)")
         )
 
-        log_sig = [sb.tile([P, SLOTS], F32, name=f"log_sig{j}") for j in range(PACK)]
+        log_sig = {part: sb.tile([P, 2, HALF], F32, name=f"log_sig{part[0]}{part[1]}") for part in parts}
+        for part in sorted(parts):
+            nc.scalar.activation(log_sig[part][:], sig_neg[part][:], ACT.Ln, bias=tiny[:])
+        ht = shared.tile([P, HT_COLS], F32, name="ht", offset=HT_AT)
+        nc.vector.memset(ht[:, PACK * SLOTS :], 0.0)
+        ht_planes = ht[:, : PACK * SLOTS].rearrange("p (j i) -> p j i", j=PACK)
+        for g, h in sorted(parts):
+            nc.vector.scalar_tensor_tensor(
+                ht_planes[:, 2 * g : 2 * g + 2, half(h)], log_sig[g, h][:], -1.0, zh[g, h][:], ALU.mult, ALU.max
+            )
+        own = [sb.tile([P, SLOTS], F32, name=f"own{j}") for j in range(PACK)]
         for j in range(PACK):
-            nc.scalar.activation(log_sig[j][:], sig_neg[j][:], ACT.Ln, bias=tiny[:])
+            nc.scalar.activation(own[j][:], ht_planes[:, j, :], ACT.Copy, scale=hsc_sb[:, j : j + 1])
+
+        sig_neg_a = sb.tile([P, SLOTS], F32, name="sig_neg_a", tag="late1", align_bytes=64)
+        nc.scalar.activation(sig_neg_a[:], neg_a[:], ACT.Sigmoid, bias=th_sb[:])
+        sig_a = sb.tile([P, SLOTS], F32, name="sig_a")
+        nc.scalar.activation(sig_a[:], neg_a[:], ACT.Sigmoid, bias=neg_th[:], scale=-1.0)
+        log_sig_a = sb.tile([P, SLOTS], F32, name="log_sig_a", tag="late0", align_bytes=64)
+        nc.scalar.activation(log_sig_a[:], sig_neg_a[:], ACT.Ln, bias=tiny[:])
 
         linked = [sb.tile([P, SLOTS], F32, name=f"linked{j}") for j in range(PACK)]
-        own = [sb.tile([P, SLOTS], F32, name=f"own{j}") for j in range(PACK)]
         hs_planes = sb.tile([P, PACK, SLOTS], BF16, name="hs_planes")
 
-        def finish_softplus(j):
-            nc.vector.scalar_tensor_tensor(ht[j][:, :SLOTS], log_sig[j][:], -1.0, zh[j][:], ALU.mult, ALU.max)
-            nc.scalar.activation(own[j][:], ht[j][:, :SLOTS], ACT.Copy, scale=hsc_sb[:, j : j + 1])
-
         def look_up(j):
-            nc.vector.tensor_copy(linked[j][:], ht[j][:].indirect(link[:]))
+            nc.vector.tensor_copy(linked[j][:], ht[:, j * SLOTS : (j + 1) * SLOTS + SPARE].indirect(link[:]))
 
         def combine(j):
             nc.vector.scalar_tensor_tensor(
                 hs_planes[:, j, :], linked[j][:], lam_hsc[:, j : j + 1], own[j][:], ALU.mult, ALU.add
             )
 
-        finish_softplus(0)
-        finish_softplus(1)
         look_up(0)
-        finish_softplus(2)
-        finish_softplus(3)
-        sig_neg_a = sb.tile([P, SLOTS], F32, name="sig_neg_a")
-        nc.scalar.activation(sig_neg_a[:], neg_a[:], ACT.Sigmoid, bias=th_sb[:])
-        sig_a = sb.tile([P, SLOTS], F32, name="sig_a")
-        nc.scalar.activation(sig_a[:], neg_a[:], ACT.Sigmoid, bias=neg_th[:], scale=-1.0)
-        log_sig_a = sb.tile([P, SLOTS], F32, name="log_sig_a")
-        nc.scalar.activation(log_sig_a[:], sig_neg_a[:], ACT.Ln, bias=tiny[:])
-        look_up(1)
-        combine(0)
-        look_up(2)
-        combine(1)
-        look_up(3)
-        combine(2)
+        for j in range(1, PACK):
+            look_up(j)
+            combine(j - 1)
+        combine(PACK - 1)
 
-        combine(3)
         neg_p = sb.tile([P, SLOTS], F32, name="neg_p")
         neg_sum = sb.tile([P, 1], F32, name="neg_sum")
         nc.vector.scalar_tensor_tensor(
             neg_p[:], neg_a[:], th_sb[:], log_sig_a[:], ALU.add, ALU.min, accum_out=neg_sum[:]
         )
-        z = sb.tile([P, 1], F32, name="z")
-        nc.vector.tensor_scalar(z[:], neg_sum[:], -1.0, reserve_sb[:], ALU.mult, ALU.add)
 
-        hs_bf = sb.tile([P, SLOTS, PACK], BF16, name="hs_bf", align_bytes=64)
+        hs_bf = [sb.tile([P, HALF, PACK], BF16, name=f"hs_bf{h}", tag=f"late{h}", align_bytes=64) for h in range(2)]
         hs_codes = sb.tile([P, SLOTS], U32, name="hs_codes", align_bytes=64)
         hs_bytes = sb.tile([P, SLOTS], U8, name="hs_bytes", align_bytes=64)
-        c0 = ps.tile([P, SLOTS], F32, name="c0")
+        c0 = [ps.tile([P, HALF], F32, name=f"c0_{h}") for h in range(2)]
 
-        def scale_and_weave(h):
-            cols = slice(h * HALF, (h + 1) * HALF)
-            nc.vector.tensor_copy(
-                hs_bf[:, cols, :].rearrange("p (c i) t -> p c t i", i=4),
-                hs_planes[:, :, cols].rearrange("p t (c i) -> p c t i", i=4),
+        def weave(copy, h):
+            copy(
+                hs_bf[h][:].rearrange("p (c i) t -> p c t i", i=4),
+                hs_planes[:, :, half(h)].rearrange("p t (c i) -> p c t i", i=4),
             )
 
         def quantise_and_multiply(h):
-            cols = slice(h * HALF, (h + 1) * HALF)
             nc.vector.quantize_mx(
-                out=hs_codes[:, cols].bitcast(FP8X4),
-                scales=hs_bytes[:, cols],
-                in_=hs_bf[:, cols, :].rearrange("p i t -> p (i t)"),
+                out=hs_codes[:, half(h)].bitcast(FP8X4),
+                scales=hs_bytes[:, half(h)],
+                in_=hs_bf[h][:].rearrange("p i t -> p (i t)"),
             )
             nc.tensor.matmul_mx(
-                out=c0[:, cols],
+                out=c0[h][:],
                 lhsT=g_codes[:].bitcast(FP8X4),
                 lhsT_scale=g_bytes[:],
-                rhs=hs_codes[:, cols].bitcast(FP8X4),
-                rhs_scale=hs_bytes[:, cols],
+                rhs=hs_codes[:, half(h)].bitcast(FP8X4),
+                rhs_scale=hs_bytes[:, half(h)],
                 start=True,
                 stop=True,
             )
 
-        scale_and_weave(0)
+        weave(nc.scalar.copy, 1)
+        weave(nc.vector.tensor_copy, 0)
+        z = sb.tile([P, 1], F32, name="z")
+        nc.vector.tensor_scalar(z[:], neg_sum[:], -1.0, reserve_sb[:], ALU.mult, ALU.add)
+        quantise_and_multiply(0)
         inv_z = sb.tile([P, 1], F32, name="inv_z")
         nc.vector.reciprocal(inv_z[:], z[:])
-        scale_and_weave(1)
-        quantise_and_multiply(0)
+        quantise_and_multiply(1)
         gain = sb.tile([P, 1], F32, name="gain")
         nc.vector.tensor_scalar(gain[:], inv_z[:], 512.0, None, ALU.mult)
-        gain_sq = sb.tile([P, 1], F32, name="gain_sq")
-        nc.vector.tensor_scalar(gain_sq[:], inv_z[:], inv_z[:], 512.0, ALU.mult, ALU.mult)
-        quantise_and_multiply(1)
+        slope = sb.tile([P, SLOTS], F32, name="slope")
+        nc.scalar.activation(slope[:], sig_a[:], ACT.Copy, scale=gain[:])
 
         terms = sb.tile([P, SLOTS], F32, name="terms")
-        dz = sb.tile([P, 1], F32, name="dz")
-        nc.vector.scalar_tensor_tensor(
-            terms[:], c0[:], gain_sq[:], neg_p[:], ALU.mult, ALU.mult, accum_out=dz[:]
-        )
-        dp = sb.tile([P, SLOTS], F32, name="dp")
-        nc.vector.tensor_scalar(dp[:], c0[:], gain[:], dz[:], ALU.mult, ALU.add)
-        nc.vector.tensor_tensor(placed[:].indirect(idx[:]), dp[:], sig_a[:], ALU.mult)
+        shift = [sb.tile([P, 1], F32, name=f"shift{h}") for h in range(2)]
+        for h in range(2):
+            nc.vector.scalar_tensor_tensor(
+                terms[:, half(h)], c0[h][:], inv_z[:], neg_p[:, half(h)], ALU.mult, ALU.mult, accum_out=shift[h][:]
+            )
+        centred = sb.tile([P, SLOTS], F32, name="centred")
+        for h in range(2):
+            nc.vector.tensor_scalar(centred[:, half(h)], c0[h][:], shift[0][:], shift[1][:], ALU.add, ALU.add)
+        nc.vector.tensor_tensor(placed[:].indirect(idx[:]), centred[:], slope[:], ALU.mult)
 
         for n in range(T // OUT_CHUNK):
             cols = slice(n * OUT_CHUNK, (n + 1) * OUT_CHUNK)

@@ -20,8 +20,12 @@ HALF = SLOTS // 2
 SPARE = 192
 CAP = 41.5
 W1_SPLIT = 84
-OUT_CHUNK = 512
-TAB_AT, KEY_AT, PLANE_AT = 0, 4 * T, 8 * T
+OUT_CHUNK = 256
+TAB_AT = 0
+W1_CODES_AT = TAB_AT + 4 * T
+KEY_AT = W1_CODES_AT + 2048
+TAB_PLANE_AT = KEY_AT - 1024
+PLANE_AT = KEY_AT + 4 * T
 Q_AT = PLANE_AT + T
 G_AT = Q_AT + 1024
 W1_AT = G_AT + 1024
@@ -61,38 +65,38 @@ def tile_attend_blrlent_capped_kernel(
                 out=pool_tile[:].bitcast(I32), in_=words[0].rearrange("p n t -> p (n t)").bitcast(I32)
             )
 
-        tab_plane = sb.tile([P, T], U8, name="tab_plane", tag="plane", align_bytes=64)
+        tab_plane = shared.tile([P, T], U8, name="tab_plane", offset=TAB_PLANE_AT)
         nc.vector.memset(tab_plane[:].bitcast(I32), 0)
-        neg_cap = shared.tile([P, 16], F32, name="neg_cap", offset=KEY_AT - 32)
+        neg_cap = shared.tile([P, 1], F32, name="neg_cap", offset=TAB_AT)
         nc.vector.memset(neg_cap[:], -CAP)
         placed = sb.tile([P, T], F32, name="placed")
         nc.vector.memset(placed[:], 0.0)
         key_plane = shared.tile([P, T], U8, name="key_plane", offset=PLANE_AT)
         nc.vector.memset(key_plane[:].bitcast(I32), 0)
         tiny = sb.tile([P, 1], F32, name="tiny")
-        nc.scalar.activation(tiny[:], neg_cap[:, 0:1], ACT.Sigmoid)
+        nc.scalar.activation(tiny[:], neg_cap[:], ACT.Sigmoid)
 
-        idx = lists.tile([P, SLOTS // 16], U16, name="idx")
-        nc.sync.dma_start(idx[:], offs)
         w1_raw = shared.tile([P, PACK, 512], F32, name="w1_raw", offset=W1_AT)
         nc.sync.dma_start(out=w1_raw[:], in_=w1.rearrange("(p t) r -> p t r", t=PACK))
+        idx = lists.tile([P, SLOTS // 16], U16, name="idx")
+        nc.sync.dma_start(idx[:], offs)
         load_scale_rows(nc.sync, tab_plane, tab_scales)
         tab_pool = shared.tile([P, T], U32, name="tab_pool", offset=TAB_AT)
         load_words(tab_pool, tab_words)
         link = lists.tile([P, SLOTS // 16], U16, name="link")
         nc.sync.dma_start(link[:], offs3)
-        key_pool = shared.tile([P, T], U32, name="key_pool", offset=KEY_AT)
-        load_words(key_pool, keys_words)
         load_scale_rows(nc.sync, key_plane, keys_scales)
 
         tab_bytes = sb.tile([P, SLOTS], U8, name="tab_bytes", align_bytes=64)
         nc.vector.tensor_copy(tab_bytes[:], tab_plane[:].indirect(idx[:]))
+        key_pool = shared.tile([P, T], U32, name="key_pool", offset=KEY_AT)
+        load_words(key_pool, keys_words)
         w1_bf = sb.tile([P, PACK, P, PACK], BF16, name="w1_bf", align_bytes=64)
         w1_dst = w1_bf[:].rearrange("p j m t -> p m t j")
         w1_src = w1_raw[:].rearrange("p t (m j) -> p m t j", j=PACK)
         nc.scalar.copy(w1_dst[:, :W1_SPLIT], w1_src[:, :W1_SPLIT])
         nc.vector.tensor_copy(w1_dst[:, W1_SPLIT:], w1_src[:, W1_SPLIT:])
-        w1_codes = sb.tile([P, 512], U32, name="w1_codes", tag="plane", align_bytes=64)
+        w1_codes = shared.tile([P, 512], U32, name="w1_codes", offset=W1_CODES_AT, align_bytes=64)
         w1_bytes = sb.tile([P, 512], U8, name="w1_bytes", align_bytes=64)
         nc.vector.quantize_mx(
             out=w1_codes[:].bitcast(FP8X4), scales=w1_bytes[:], in_=w1_bf[:].rearrange("p j m t -> p (j m t)")
@@ -105,13 +109,13 @@ def tile_attend_blrlent_capped_kernel(
         nc.sync.dma_start(out=q_raw[:], in_=query.rearrange("(p t) q -> p t q", t=PACK))
         g_raw = shared.tile([P, PACK, P], F32, name="g_raw", offset=W1_AT + 2048)
         nc.sync.dma_start(out=g_raw[:], in_=gout.rearrange("(p t) q -> p t q", t=PACK))
-        lam_sb = shared.tile([P, PACK], F32, name="lam_sb", offset=W1_AT + 4096)
+        lam_sb = shared.tile([P, PACK], F32, name="lam_sb", offset=TAB_AT + 1024)
         nc.sync.dma_start(out=lam_sb[:], in_=lam.rearrange("(p j) o -> p (j o)", j=PACK))
-        hsc_sb = shared.tile([P, PACK], F32, name="hsc_sb", offset=W1_AT + 4096 + 64)
+        hsc_sb = shared.tile([P, PACK], F32, name="hsc_sb", offset=TAB_AT + 1024 + 64)
         nc.sync.dma_start(out=hsc_sb[:], in_=hsc.rearrange("(p j) o -> p (j o)", j=PACK))
-        th_sb = shared.tile([P, 1], F32, name="th_sb", offset=W1_AT + 4096 + 128)
+        th_sb = shared.tile([P, 1], F32, name="th_sb", offset=TAB_AT + 1024 + 128)
         nc.sync.dma_start(out=th_sb[:], in_=th)
-        reserve_sb = shared.tile([P, 1], F32, name="reserve_sb", offset=W1_AT + 4096 + 192)
+        reserve_sb = shared.tile([P, 1], F32, name="reserve_sb", offset=TAB_AT + 1024 + 192)
         nc.sync.dma_start(out=reserve_sb[:], in_=reserve)
 
         parts = [(g, h) for h in range(2) for g in range(2)]
@@ -132,10 +136,10 @@ def tile_attend_blrlent_capped_kernel(
             nc.scalar.activation(sig_neg[g, h][:], zh[g, h][:], ACT.Sigmoid, scale=-1.0)
 
         q_bf = shared.tile([P, P, PACK], BF16, name="q_bf", offset=Q_AT, align_bytes=64)
-        key_bytes = sb.tile([P, SLOTS], U8, name="key_bytes", align_bytes=64)
+        key_bytes = shared.tile([P, SLOTS], U8, name="key_bytes", offset=TAB_AT, align_bytes=64)
+        nc.vector.tensor_copy(key_bytes[:], key_plane[:].indirect(idx[:]))
         key_codes = sb.tile([P, SLOTS], U32, name="key_codes", align_bytes=64)
         nc.vector.tensor_copy(key_codes[:], key_pool[:].indirect(idx[:]))
-        nc.vector.tensor_copy(key_bytes[:], key_plane[:].indirect(idx[:]))
         nc.vector.tensor_scalar(
             q_bf[:].rearrange("p (c i) t -> p c t i", i=4),
             q_raw[:].rearrange("p t (c i) -> p c t i", i=4),
@@ -168,7 +172,7 @@ def tile_attend_blrlent_capped_kernel(
         lam_hsc = sb.tile([P, PACK], F32, name="lam_hsc")
         nc.gpsimd.tensor_tensor(lam_hsc[:], lam_sb[:], hsc_sb[:], ALU.mult)
 
-        old_sb = shared.tile([P, T], F32, name="old_sb", offset=TAB_AT)
+        old_sb = shared.tile([P, T], F32, name="old_sb", offset=W1_AT)
         nc.sync.dma_start(out=old_sb[:], in_=old)
 
         g_codes = sb.tile([P, P], U32, name="g_codes", align_bytes=64)
@@ -178,17 +182,28 @@ def tile_attend_blrlent_capped_kernel(
         )
 
         log_sig = {part: sb.tile([P, 2, HALF], F32, name=f"log_sig{part[0]}{part[1]}") for part in parts}
-        for part in sorted(parts):
-            nc.scalar.activation(log_sig[part][:], sig_neg[part][:], ACT.Ln, bias=tiny[:])
         ht = shared.tile([P, HT_COLS], F32, name="ht", offset=HT_AT)
         nc.vector.memset(ht[:, PACK * SLOTS :], 0.0)
         ht_planes = ht[:, : PACK * SLOTS].rearrange("p (j i) -> p j i", j=PACK)
-        for g, h in sorted(parts):
+        pieces = [(0, 0, 0, 1), (0, 0, 1, 2), (0, 1, 0, 2), (1, 0, 0, 2), (1, 1, 0, 2)]
+        for g, h, lo, hi in pieces:
+            nc.scalar.activation(log_sig[g, h][:, lo:hi, :], sig_neg[g, h][:, lo:hi, :], ACT.Ln, bias=tiny[:])
+        for g, h, lo, hi in pieces:
             nc.vector.scalar_tensor_tensor(
-                ht_planes[:, 2 * g : 2 * g + 2, half(h)], log_sig[g, h][:], -1.0, zh[g, h][:], ALU.mult, ALU.max
+                ht_planes[:, 2 * g + lo : 2 * g + hi, half(h)],
+                log_sig[g, h][:, lo:hi, :],
+                -1.0,
+                zh[g, h][:, lo:hi, :],
+                ALU.mult,
+                ALU.max,
             )
         own = [sb.tile([P, SLOTS], F32, name=f"own{j}") for j in range(PACK)]
-        for j in range(PACK):
+        for h in range(2):
+            for j in range(2):
+                nc.gpsimd.tensor_scalar(
+                    own[j][:, half(h)], ht_planes[:, j, half(h)], hsc_sb[:, j : j + 1], 0.0, ALU.mult, ALU.add
+                )
+        for j in range(2, PACK):
             nc.scalar.activation(own[j][:], ht_planes[:, j, :], ACT.Copy, scale=hsc_sb[:, j : j + 1])
 
         sig_neg_a = sb.tile([P, SLOTS], F32, name="sig_neg_a", tag="late1", align_bytes=64)
@@ -204,16 +219,31 @@ def tile_attend_blrlent_capped_kernel(
         def look_up(j):
             nc.vector.tensor_copy(linked[j][:], ht[:, j * SLOTS : (j + 1) * SLOTS + SPARE].indirect(link[:]))
 
-        def combine(j):
+        def combine(j, cols):
             nc.vector.scalar_tensor_tensor(
-                hs_planes[:, j, :], linked[j][:], lam_hsc[:, j : j + 1], own[j][:], ALU.mult, ALU.add
+                hs_planes[:, j, cols], linked[j][:, cols], lam_hsc[:, j : j + 1], own[j][:, cols], ALU.mult, ALU.add
             )
 
         look_up(0)
         for j in range(1, PACK):
             look_up(j)
-            combine(j - 1)
-        combine(PACK - 1)
+            combine(j - 1, slice(0, SLOTS))
+        combine(PACK - 1, half(0))
+        combine(PACK - 1, half(1))
+
+        hs_bf = [
+            sb.tile([P, HALF, PACK], BF16, name="hs_bf0", align_bytes=64),
+            sb.tile([P, HALF, PACK], BF16, name="hs_bf1", tag="late1", align_bytes=64),
+        ]
+
+        def weave(copy, h):
+            copy(
+                hs_bf[h][:].rearrange("p (c i) t -> p c t i", i=4),
+                hs_planes[:, :, half(h)].rearrange("p t (c i) -> p c t i", i=4),
+            )
+
+        weave(nc.vector.tensor_copy, 0)
+        weave(nc.scalar.copy, 1)
 
         neg_p = sb.tile([P, SLOTS], F32, name="neg_p")
         neg_sum = sb.tile([P, 1], F32, name="neg_sum")
@@ -221,16 +251,9 @@ def tile_attend_blrlent_capped_kernel(
             neg_p[:], neg_a[:], th_sb[:], log_sig_a[:], ALU.add, ALU.min, accum_out=neg_sum[:]
         )
 
-        hs_bf = [sb.tile([P, HALF, PACK], BF16, name=f"hs_bf{h}", tag=f"late{h}", align_bytes=64) for h in range(2)]
-        hs_codes = sb.tile([P, SLOTS], U32, name="hs_codes", align_bytes=64)
+        hs_codes = sb.tile([P, SLOTS], U32, name="hs_codes", tag="late0", align_bytes=64)
         hs_bytes = sb.tile([P, SLOTS], U8, name="hs_bytes", align_bytes=64)
         c0 = [ps.tile([P, HALF], F32, name=f"c0_{h}") for h in range(2)]
-
-        def weave(copy, h):
-            copy(
-                hs_bf[h][:].rearrange("p (c i) t -> p c t i", i=4),
-                hs_planes[:, :, half(h)].rearrange("p t (c i) -> p c t i", i=4),
-            )
 
         def quantise_and_multiply(h):
             nc.vector.quantize_mx(
@@ -248,14 +271,12 @@ def tile_attend_blrlent_capped_kernel(
                 stop=True,
             )
 
-        weave(nc.scalar.copy, 1)
-        weave(nc.vector.tensor_copy, 0)
+        quantise_and_multiply(0)
         z = sb.tile([P, 1], F32, name="z")
         nc.vector.tensor_scalar(z[:], neg_sum[:], -1.0, reserve_sb[:], ALU.mult, ALU.add)
-        quantise_and_multiply(0)
+        quantise_and_multiply(1)
         inv_z = sb.tile([P, 1], F32, name="inv_z")
         nc.vector.reciprocal(inv_z[:], z[:])
-        quantise_and_multiply(1)
         gain = sb.tile([P, 1], F32, name="gain")
         nc.vector.tensor_scalar(gain[:], inv_z[:], 512.0, None, ALU.mult)
         slope = sb.tile([P, SLOTS], F32, name="slope")

@@ -188,7 +188,11 @@ def tile_attend_blrlent_capped_kernel(
         pieces = [(0, 0, 0, 1), (0, 0, 1, 2), (0, 1, 0, 2), (1, 0, 0, 2), (1, 1, 0, 2)]
         for g, h, lo, hi in pieces:
             nc.scalar.activation(log_sig[g, h][:, lo:hi, :], sig_neg[g, h][:, lo:hi, :], ACT.Ln, bias=tiny[:])
-        for g, h, lo, hi in pieces:
+        linked = [sb.tile([P, SLOTS], F32, name=f"linked{j}") for j in range(PACK)]
+        own = [sb.tile([P, SLOTS], F32, name=f"own{j}") for j in range(PACK)]
+        hs_planes = sb.tile([P, PACK, SLOTS], BF16, name="hs_planes")
+
+        def finish(g, h, lo, hi):
             nc.vector.scalar_tensor_tensor(
                 ht_planes[:, 2 * g + lo : 2 * g + hi, half(h)],
                 log_sig[g, h][:, lo:hi, :],
@@ -197,12 +201,32 @@ def tile_attend_blrlent_capped_kernel(
                 ALU.mult,
                 ALU.max,
             )
-        own = [sb.tile([P, SLOTS], F32, name=f"own{j}") for j in range(PACK)]
+
+        def look_up(j):
+            nc.vector.tensor_copy(linked[j][:], ht[:, j * SLOTS : (j + 1) * SLOTS + SPARE].indirect(link[:]))
+
+        def combine(j, cols):
+            nc.vector.scalar_tensor_tensor(
+                hs_planes[:, j, cols], linked[j][:, cols], lam_hsc[:, j : j + 1], own[j][:, cols], ALU.mult, ALU.add
+            )
+
+        for piece in pieces[:3]:
+            finish(*piece)
+        look_up(0)
+        for piece in pieces[3:]:
+            finish(*piece)
+        for j in range(1, PACK):
+            look_up(j)
+
         for h in range(2):
             for j in range(2):
                 nc.gpsimd.tensor_scalar(
                     own[j][:, half(h)], ht_planes[:, j, half(h)], hsc_sb[:, j : j + 1], 0.0, ALU.mult, ALU.add
                 )
+        for j in range(2):
+            scaled = sb.tile([P, SLOTS], F32, name=f"scaled{j}")
+            nc.gpsimd.tensor_scalar(scaled[:], linked[j][:], lam_hsc[:, j : j + 1], 0.0, ALU.mult, ALU.add)
+            nc.gpsimd.tensor_tensor(hs_planes[:, j, :], scaled[:], own[j][:], ALU.add)
         for j in range(2, PACK):
             nc.scalar.activation(own[j][:], ht_planes[:, j, :], ACT.Copy, scale=hsc_sb[:, j : j + 1])
 
@@ -213,21 +237,7 @@ def tile_attend_blrlent_capped_kernel(
         log_sig_a = sb.tile([P, SLOTS], F32, name="log_sig_a", tag="late0", align_bytes=64)
         nc.scalar.activation(log_sig_a[:], sig_neg_a[:], ACT.Ln, bias=tiny[:])
 
-        linked = [sb.tile([P, SLOTS], F32, name=f"linked{j}") for j in range(PACK)]
-        hs_planes = sb.tile([P, PACK, SLOTS], BF16, name="hs_planes")
-
-        def look_up(j):
-            nc.vector.tensor_copy(linked[j][:], ht[:, j * SLOTS : (j + 1) * SLOTS + SPARE].indirect(link[:]))
-
-        def combine(j, cols):
-            nc.vector.scalar_tensor_tensor(
-                hs_planes[:, j, cols], linked[j][:, cols], lam_hsc[:, j : j + 1], own[j][:, cols], ALU.mult, ALU.add
-            )
-
-        look_up(0)
-        for j in range(1, PACK):
-            look_up(j)
-            combine(j - 1, slice(0, SLOTS))
+        combine(PACK - 2, slice(0, SLOTS))
         combine(PACK - 1, half(0))
         combine(PACK - 1, half(1))
 

@@ -14,25 +14,31 @@ ACT = mybir.ActivationFunctionType
 
 P = 128
 PACK = 4
+HIDDEN = P * PACK
 T = 2048
 SLOTS = 512
 HALF = SLOTS // 2
-SPARE = 192
+RUN = 4
+GRAD_SCALE = 512.0
 CAP = 41.5
+SPARE = 192
 W1_SPLIT = 84
 OUT_CHUNK = 256
+
 TAB_AT = 0
+VECTORS_AT = TAB_AT + 1024
+VECTOR_PITCH = 64
 W1_CODES_AT = TAB_AT + 4 * T
-KEY_AT = W1_CODES_AT + 2048
-TAB_PLANE_AT = KEY_AT - 1024
-PLANE_AT = KEY_AT + 4 * T
-Q_AT = PLANE_AT + T
-G_AT = Q_AT + 1024
-W1_AT = G_AT + 1024
+KEY_AT = W1_CODES_AT + 4 * HIDDEN
+TAB_PLANE_AT = KEY_AT - T // 2
+KEY_PLANE_AT = KEY_AT + 4 * T
+Q_AT = KEY_PLANE_AT + T
+G_AT = Q_AT + 2 * P * PACK
+W1_AT = G_AT + 2 * P * PACK
 HT_COLS = PACK * SLOTS + SPARE
 HT_AT = W1_AT - 4 * HT_COLS
 
-FLOPS = 2 * 512 * 512 * (128 + 512 + 128)
+FLOPS = 2 * 512 * SLOTS * (P + HIDDEN + P)
 
 
 def half(h):
@@ -53,16 +59,34 @@ def tile_attend_blrlent_capped_kernel(
         shared = ctx.enter_context(tc.tile_pool(name="shared", bufs=1))
         ps = ctx.enter_context(tc.psum_pool(name="ps", bufs=1))
 
-        def load_scale_rows(queue, plane, scales):
+        def load_scale_rows(scale_tile, scales):
             for quad in range(4):
-                queue.dma_start(
-                    out=plane[32 * quad : 32 * quad + 4, :].bitcast(I32),
+                nc.sync.dma_start(
+                    out=scale_tile[32 * quad : 32 * quad + 4, :].bitcast(I32),
                     in_=scales[0, 4 * quad : 4 * quad + 4, :].bitcast(I32),
                 )
 
-        def load_words(pool_tile, words):
-            nc.sync.dma_start(
-                out=pool_tile[:].bitcast(I32), in_=words[0].rearrange("p n t -> p (n t)").bitcast(I32)
+        def load_words(word_tile, words):
+            nc.sync.dma_start(out=word_tile[:].bitcast(I32), in_=words[0].rearrange("p n t -> p (n t)").bitcast(I32))
+
+        def woven(tile):
+            return tile.rearrange("p (c i) t -> p c t i", i=RUN)
+
+        def rows(tile):
+            return tile.rearrange("p t (c i) -> p c t i", i=RUN)
+
+        def quantise(codes, scale_bytes, values):
+            nc.vector.quantize_mx(out=codes.bitcast(FP8X4), scales=scale_bytes, in_=values)
+
+        def multiply(result, left_codes, left_bytes, right_codes, right_bytes):
+            nc.tensor.matmul_mx(
+                out=result,
+                lhsT=left_codes.bitcast(FP8X4),
+                lhsT_scale=left_bytes,
+                rhs=right_codes.bitcast(FP8X4),
+                rhs_scale=right_bytes,
+                start=True,
+                stop=True,
             )
 
         tab_plane = shared.tile([P, T], U8, name="tab_plane", offset=TAB_PLANE_AT)
@@ -71,21 +95,21 @@ def tile_attend_blrlent_capped_kernel(
         nc.vector.memset(neg_cap[:], -CAP)
         placed = sb.tile([P, T], F32, name="placed")
         nc.vector.memset(placed[:], 0.0)
-        key_plane = shared.tile([P, T], U8, name="key_plane", offset=PLANE_AT)
+        key_plane = shared.tile([P, T], U8, name="key_plane", offset=KEY_PLANE_AT)
         nc.vector.memset(key_plane[:].bitcast(I32), 0)
         tiny = sb.tile([P, 1], F32, name="tiny")
         nc.scalar.activation(tiny[:], neg_cap[:], ACT.Sigmoid)
 
-        w1_raw = shared.tile([P, PACK, 512], F32, name="w1_raw", offset=W1_AT)
+        w1_raw = shared.tile([P, PACK, HIDDEN], F32, name="w1_raw", offset=W1_AT)
         nc.sync.dma_start(out=w1_raw[:], in_=w1.rearrange("(p t) r -> p t r", t=PACK))
         idx = lists.tile([P, SLOTS // 16], U16, name="idx")
         nc.sync.dma_start(idx[:], offs)
-        load_scale_rows(nc.sync, tab_plane, tab_scales)
+        load_scale_rows(tab_plane, tab_scales)
         tab_pool = shared.tile([P, T], U32, name="tab_pool", offset=TAB_AT)
         load_words(tab_pool, tab_words)
         link = lists.tile([P, SLOTS // 16], U16, name="link")
         nc.sync.dma_start(link[:], offs3)
-        load_scale_rows(nc.sync, key_plane, keys_scales)
+        load_scale_rows(key_plane, keys_scales)
 
         tab_bytes = sb.tile([P, SLOTS], U8, name="tab_bytes", align_bytes=64)
         nc.vector.tensor_copy(tab_bytes[:], tab_plane[:].indirect(idx[:]))
@@ -96,26 +120,24 @@ def tile_attend_blrlent_capped_kernel(
         w1_src = w1_raw[:].rearrange("p t (m j) -> p m t j", j=PACK)
         nc.scalar.copy(w1_dst[:, :W1_SPLIT], w1_src[:, :W1_SPLIT])
         nc.vector.tensor_copy(w1_dst[:, W1_SPLIT:], w1_src[:, W1_SPLIT:])
-        w1_codes = shared.tile([P, 512], U32, name="w1_codes", offset=W1_CODES_AT, align_bytes=64)
-        w1_bytes = sb.tile([P, 512], U8, name="w1_bytes", align_bytes=64)
-        nc.vector.quantize_mx(
-            out=w1_codes[:].bitcast(FP8X4), scales=w1_bytes[:], in_=w1_bf[:].rearrange("p j m t -> p (j m t)")
-        )
+        w1_codes = shared.tile([P, HIDDEN], U32, name="w1_codes", offset=W1_CODES_AT, align_bytes=64)
+        w1_bytes = sb.tile([P, HIDDEN], U8, name="w1_bytes", align_bytes=64)
+        quantise(w1_codes[:], w1_bytes[:], w1_bf[:].rearrange("p j m t -> p (j m t)"))
         tab_codes = sb.tile([P, SLOTS], U32, name="tab_codes", align_bytes=64)
         for h in range(2):
             nc.vector.tensor_copy(tab_codes[:, half(h)], tab_pool[:].indirect(idx[:, half_list(h)]))
 
         q_raw = shared.tile([P, PACK, P], F32, name="q_raw", offset=W1_AT)
         nc.sync.dma_start(out=q_raw[:], in_=query.rearrange("(p t) q -> p t q", t=PACK))
-        g_raw = shared.tile([P, PACK, P], F32, name="g_raw", offset=W1_AT + 2048)
+        g_raw = shared.tile([P, PACK, P], F32, name="g_raw", offset=W1_AT + 4 * PACK * P)
         nc.sync.dma_start(out=g_raw[:], in_=gout.rearrange("(p t) q -> p t q", t=PACK))
-        lam_sb = shared.tile([P, PACK], F32, name="lam_sb", offset=TAB_AT + 1024)
+        lam_sb = shared.tile([P, PACK], F32, name="lam_sb", offset=VECTORS_AT)
         nc.sync.dma_start(out=lam_sb[:], in_=lam.rearrange("(p j) o -> p (j o)", j=PACK))
-        hsc_sb = shared.tile([P, PACK], F32, name="hsc_sb", offset=TAB_AT + 1024 + 64)
+        hsc_sb = shared.tile([P, PACK], F32, name="hsc_sb", offset=VECTORS_AT + VECTOR_PITCH)
         nc.sync.dma_start(out=hsc_sb[:], in_=hsc.rearrange("(p j) o -> p (j o)", j=PACK))
-        th_sb = shared.tile([P, 1], F32, name="th_sb", offset=TAB_AT + 1024 + 128)
+        th_sb = shared.tile([P, 1], F32, name="th_sb", offset=VECTORS_AT + 2 * VECTOR_PITCH)
         nc.sync.dma_start(out=th_sb[:], in_=th)
-        reserve_sb = shared.tile([P, 1], F32, name="reserve_sb", offset=TAB_AT + 1024 + 192)
+        reserve_sb = shared.tile([P, 1], F32, name="reserve_sb", offset=VECTORS_AT + 3 * VECTOR_PITCH)
         nc.sync.dma_start(out=reserve_sb[:], in_=reserve)
 
         parts = [(g, h) for h in range(2) for g in range(2)]
@@ -123,15 +145,13 @@ def tile_attend_blrlent_capped_kernel(
         sig_neg = {part: sb.tile([P, 2, HALF], F32, name=f"sig_neg{part[0]}{part[1]}") for part in parts}
         for g, h in parts:
             for e in range(2):
-                cols = slice((2 * g + e) * P, (2 * g + e + 1) * P)
-                nc.tensor.matmul_mx(
-                    out=zh[g, h][:, e, :],
-                    lhsT=w1_codes[:, cols].bitcast(FP8X4),
-                    lhsT_scale=w1_bytes[:, cols],
-                    rhs=tab_codes[:, half(h)].bitcast(FP8X4),
-                    rhs_scale=tab_bytes[:, half(h)],
-                    start=True,
-                    stop=True,
+                features = slice((2 * g + e) * P, (2 * g + e + 1) * P)
+                multiply(
+                    zh[g, h][:, e, :],
+                    w1_codes[:, features],
+                    w1_bytes[:, features],
+                    tab_codes[:, half(h)],
+                    tab_bytes[:, half(h)],
                 )
             nc.scalar.activation(sig_neg[g, h][:], zh[g, h][:], ACT.Sigmoid, scale=-1.0)
 
@@ -140,59 +160,39 @@ def tile_attend_blrlent_capped_kernel(
         nc.vector.tensor_copy(key_bytes[:], key_plane[:].indirect(idx[:]))
         key_codes = sb.tile([P, SLOTS], U32, name="key_codes", align_bytes=64)
         nc.vector.tensor_copy(key_codes[:], key_pool[:].indirect(idx[:]))
-        nc.vector.tensor_scalar(
-            q_bf[:].rearrange("p (c i) t -> p c t i", i=4),
-            q_raw[:].rearrange("p t (c i) -> p c t i", i=4),
-            -1.0,
-            None,
-            ALU.mult,
-        )
+        nc.vector.tensor_scalar(woven(q_bf[:]), rows(q_raw[:]), -1.0, None, ALU.mult)
         g_bf = shared.tile([P, P, PACK], BF16, name="g_bf", offset=G_AT, align_bytes=64)
-        nc.vector.tensor_copy(
-            g_bf[:].rearrange("p (c i) t -> p c t i", i=4), g_raw[:].rearrange("p t (c i) -> p c t i", i=4)
-        )
+        nc.vector.tensor_copy(woven(g_bf[:]), rows(g_raw[:]))
         q_codes = sb.tile([P, P], U32, name="q_codes", align_bytes=64)
         q_bytes = sb.tile([P, P], U8, name="q_bytes", align_bytes=64)
-        nc.vector.quantize_mx(
-            out=q_codes[:].bitcast(FP8X4), scales=q_bytes[:], in_=q_bf[:].rearrange("p q t -> p (q t)")
-        )
+        quantise(q_codes[:], q_bytes[:], q_bf[:].rearrange("p q t -> p (q t)"))
         neg_a = ps.tile([P, SLOTS], F32, name="neg_a")
-        nc.tensor.matmul_mx(
-            out=neg_a[:],
-            lhsT=q_codes[:].bitcast(FP8X4),
-            lhsT_scale=q_bytes[:],
-            rhs=key_codes[:].bitcast(FP8X4),
-            rhs_scale=key_bytes[:],
-            start=True,
-            stop=True,
-        )
+        multiply(neg_a[:], q_codes[:], q_bytes[:], key_codes[:], key_bytes[:])
+
         neg_th = sb.tile([P, 1], F32, name="neg_th")
         nc.gpsimd.tensor_scalar(neg_th[:], th_sb[:], -1.0, 0.0, ALU.mult, ALU.add)
-
         lam_hsc = sb.tile([P, PACK], F32, name="lam_hsc")
         nc.gpsimd.tensor_tensor(lam_hsc[:], lam_sb[:], hsc_sb[:], ALU.mult)
-
         old_sb = shared.tile([P, T], F32, name="old_sb", offset=W1_AT)
         nc.sync.dma_start(out=old_sb[:], in_=old)
-
         g_codes = sb.tile([P, P], U32, name="g_codes", align_bytes=64)
         g_bytes = sb.tile([P, P], U8, name="g_bytes", align_bytes=64)
-        nc.vector.quantize_mx(
-            out=g_codes[:].bitcast(FP8X4), scales=g_bytes[:], in_=g_bf[:].rearrange("p q t -> p (q t)")
-        )
+        quantise(g_codes[:], g_bytes[:], g_bf[:].rearrange("p q t -> p (q t)"))
 
         log_sig = {part: sb.tile([P, 2, HALF], F32, name=f"log_sig{part[0]}{part[1]}") for part in parts}
         ht = shared.tile([P, HT_COLS], F32, name="ht", offset=HT_AT)
         nc.vector.memset(ht[:, PACK * SLOTS :], 0.0)
         ht_planes = ht[:, : PACK * SLOTS].rearrange("p (j i) -> p j i", j=PACK)
-        pieces = [(0, 0, 0, 1), (0, 0, 1, 2), (0, 1, 0, 2), (1, 0, 0, 2), (1, 1, 0, 2)]
-        for g, h, lo, hi in pieces:
+        first_pair = [(0, 0, 0, 1), (0, 0, 1, 2), (0, 1, 0, 2)]
+        second_pair = [(1, 0, 0, 2), (1, 1, 0, 2)]
+        for g, h, lo, hi in first_pair + second_pair:
             nc.scalar.activation(log_sig[g, h][:, lo:hi, :], sig_neg[g, h][:, lo:hi, :], ACT.Ln, bias=tiny[:])
+
         linked = [sb.tile([P, SLOTS], F32, name=f"linked{j}") for j in range(PACK)]
         own = [sb.tile([P, SLOTS], F32, name=f"own{j}") for j in range(PACK)]
         hs_planes = sb.tile([P, PACK, SLOTS], BF16, name="hs_planes")
 
-        def finish(g, h, lo, hi):
+        def finish_softplus(g, h, lo, hi):
             nc.vector.scalar_tensor_tensor(
                 ht_planes[:, 2 * g + lo : 2 * g + hi, half(h)],
                 log_sig[g, h][:, lo:hi, :],
@@ -205,16 +205,16 @@ def tile_attend_blrlent_capped_kernel(
         def look_up(j):
             nc.vector.tensor_copy(linked[j][:], ht[:, j * SLOTS : (j + 1) * SLOTS + SPARE].indirect(link[:]))
 
-        def combine(j, cols):
+        def combine(j, slots):
             nc.vector.scalar_tensor_tensor(
-                hs_planes[:, j, cols], linked[j][:, cols], lam_hsc[:, j : j + 1], own[j][:, cols], ALU.mult, ALU.add
+                hs_planes[:, j, slots], linked[j][:, slots], lam_hsc[:, j : j + 1], own[j][:, slots], ALU.mult, ALU.add
             )
 
-        for piece in pieces[:3]:
-            finish(*piece)
+        for piece in first_pair:
+            finish_softplus(*piece)
         look_up(0)
-        for piece in pieces[3:]:
-            finish(*piece)
+        for piece in second_pair:
+            finish_softplus(*piece)
         for j in range(1, PACK):
             look_up(j)
 
@@ -223,10 +223,9 @@ def tile_attend_blrlent_capped_kernel(
                 nc.gpsimd.tensor_scalar(
                     own[j][:, half(h)], ht_planes[:, j, half(h)], hsc_sb[:, j : j + 1], 0.0, ALU.mult, ALU.add
                 )
-        for j in range(2):
-            scaled = sb.tile([P, SLOTS], F32, name=f"scaled{j}")
-            nc.gpsimd.tensor_scalar(scaled[:], linked[j][:], lam_hsc[:, j : j + 1], 0.0, ALU.mult, ALU.add)
-            nc.gpsimd.tensor_tensor(hs_planes[:, j, :], scaled[:], own[j][:], ALU.add)
+        scaled = sb.tile([P, SLOTS], F32, name="scaled")
+        nc.gpsimd.tensor_scalar(scaled[:], linked[0][:], lam_hsc[:, 0:1], 0.0, ALU.mult, ALU.add)
+        nc.gpsimd.tensor_tensor(hs_planes[:, 0, :], scaled[:], own[0][:], ALU.add)
         for j in range(2, PACK):
             nc.scalar.activation(own[j][:], ht_planes[:, j, :], ACT.Copy, scale=hsc_sb[:, j : j + 1])
 
@@ -237,23 +236,17 @@ def tile_attend_blrlent_capped_kernel(
         log_sig_a = sb.tile([P, SLOTS], F32, name="log_sig_a", tag="late0", align_bytes=64)
         nc.scalar.activation(log_sig_a[:], sig_neg_a[:], ACT.Ln, bias=tiny[:])
 
-        combine(PACK - 2, slice(0, SLOTS))
-        combine(PACK - 1, half(0))
-        combine(PACK - 1, half(1))
+        for j in range(1, PACK - 1):
+            combine(j, slice(0, SLOTS))
+        for h in range(2):
+            combine(PACK - 1, half(h))
 
         hs_bf = [
             sb.tile([P, HALF, PACK], BF16, name="hs_bf0", align_bytes=64),
             sb.tile([P, HALF, PACK], BF16, name="hs_bf1", tag="late1", align_bytes=64),
         ]
-
-        def weave(copy, h):
-            copy(
-                hs_bf[h][:].rearrange("p (c i) t -> p c t i", i=4),
-                hs_planes[:, :, half(h)].rearrange("p t (c i) -> p c t i", i=4),
-            )
-
-        weave(nc.vector.tensor_copy, 0)
-        weave(nc.scalar.copy, 1)
+        nc.vector.tensor_copy(woven(hs_bf[0][:]), rows(hs_planes[:, :, half(0)]))
+        nc.scalar.copy(woven(hs_bf[1][:]), rows(hs_planes[:, :, half(1)]))
 
         neg_p = sb.tile([P, SLOTS], F32, name="neg_p")
         neg_sum = sb.tile([P, 1], F32, name="neg_sum")
@@ -266,20 +259,8 @@ def tile_attend_blrlent_capped_kernel(
         c0 = [ps.tile([P, HALF], F32, name=f"c0_{h}") for h in range(2)]
 
         def quantise_and_multiply(h):
-            nc.vector.quantize_mx(
-                out=hs_codes[:, half(h)].bitcast(FP8X4),
-                scales=hs_bytes[:, half(h)],
-                in_=hs_bf[h][:].rearrange("p i t -> p (i t)"),
-            )
-            nc.tensor.matmul_mx(
-                out=c0[h][:],
-                lhsT=g_codes[:].bitcast(FP8X4),
-                lhsT_scale=g_bytes[:],
-                rhs=hs_codes[:, half(h)].bitcast(FP8X4),
-                rhs_scale=hs_bytes[:, half(h)],
-                start=True,
-                stop=True,
-            )
+            quantise(hs_codes[:, half(h)], hs_bytes[:, half(h)], hs_bf[h][:].rearrange("p i t -> p (i t)"))
+            multiply(c0[h][:], g_codes[:], g_bytes[:], hs_codes[:, half(h)], hs_bytes[:, half(h)])
 
         quantise_and_multiply(0)
         z = sb.tile([P, 1], F32, name="z")
@@ -288,7 +269,7 @@ def tile_attend_blrlent_capped_kernel(
         inv_z = sb.tile([P, 1], F32, name="inv_z")
         nc.vector.reciprocal(inv_z[:], z[:])
         gain = sb.tile([P, 1], F32, name="gain")
-        nc.vector.tensor_scalar(gain[:], inv_z[:], 512.0, None, ALU.mult)
+        nc.vector.tensor_scalar(gain[:], inv_z[:], GRAD_SCALE, None, ALU.mult)
         slope = sb.tile([P, SLOTS], F32, name="slope")
         nc.scalar.activation(slope[:], sig_a[:], ACT.Copy, scale=gain[:])
 
@@ -304,8 +285,8 @@ def tile_attend_blrlent_capped_kernel(
         nc.vector.tensor_tensor(placed[:].indirect(idx[:]), centred[:], slope[:], ALU.mult)
 
         for n in range(T // OUT_CHUNK):
-            cols = slice(n * OUT_CHUNK, (n + 1) * OUT_CHUNK)
+            tokens = slice(n * OUT_CHUNK, (n + 1) * OUT_CHUNK)
             total = sb.tile([P, OUT_CHUNK], F32, name=f"total{n}")
-            nc.vector.tensor_tensor(total[:], placed[:, cols], old_sb[:, cols], ALU.add)
+            nc.vector.tensor_tensor(total[:], placed[:, tokens], old_sb[:, tokens], ALU.add)
             queue = nc.sync if n % 2 == 0 else nc.scalar
-            queue.dma_start(out=out[:, cols], in_=total[:])
+            queue.dma_start(out=out[:, tokens], in_=total[:])

from contextlib import ExitStack

import concourse.mybir as mybir

F32 = mybir.dt.float32
BF16 = mybir.dt.bfloat16
I32 = mybir.dt.int32
U32 = mybir.dt.uint32
U16 = mybir.dt.uint16
U8 = mybir.dt.uint8
FP8X4 = mybir.dt.float8_e4m3fn_x4
ALU = mybir.AluOpType
ACT = mybir.ActivationFunctionType

P = 128
PACK = 4
HIDDEN = P * PACK
T = 2048
SLOTS = 512
HALF = SLOTS // 2
RUN = 4
GRAD_SCALE = 512.0
CAP = 41.5
SPARE = 192
W1_SPLIT = 84
OUT_CHUNK = 256

TAB_AT = 0
VECTORS_AT = TAB_AT + 1024
VECTOR_PITCH = 64
W1_CODES_AT = TAB_AT + 4 * T
KEY_AT = W1_CODES_AT + 4 * HIDDEN
TAB_PLANE_AT = KEY_AT - T // 2
KEY_PLANE_AT = KEY_AT + 4 * T
Q_AT = KEY_PLANE_AT + T
G_AT = Q_AT + 2 * P * PACK
W1_AT = G_AT + 2 * P * PACK
HT_COLS = PACK * SLOTS + SPARE
HT_AT = W1_AT - 4 * HT_COLS

FLOPS = 2 * 512 * SLOTS * (P + HIDDEN + P)


def half(h):
    return slice(h * HALF, (h + 1) * HALF)


def half_list(h):
    return slice(h * HALF // 16, (h + 1) * HALF // 16)


def tile_attend_blrlent_capped_kernel(
    tc, query, keys_words, keys_scales, th, reserve, tab_words, tab_scales, w1, lam, gout, hsc, old, offs3, offs, out
):
    nc = tc.nc
    with ExitStack() as ctx:
        lists = ctx.enter_context(tc.tile_pool(name="lists", bufs=1))
        sb = ctx.enter_context(tc.tile_pool(name="sb", bufs=1))
        shared = ctx.enter_context(tc.tile_pool(name="shared", bufs=1))
        ps = ctx.enter_context(tc.psum_pool(name="ps", bufs=1))

        def load_scale_rows(scale_tile, scales):
            for quad in range(4):
                nc.sync.dma_start(
                    out=scale_tile[32 * quad : 32 * quad + 4, :].bitcast(I32),
                    in_=scales[0, 4 * quad : 4 * quad + 4, :].bitcast(I32),
                )

        def load_words(word_tile, words):
            nc.sync.dma_start(out=word_tile[:].bitcast(I32), in_=words[0].rearrange("p n t -> p (n t)").bitcast(I32))

        def woven(tile):
            return tile.rearrange("p (c i) t -> p c t i", i=RUN)

        def rows(tile):
            return tile.rearrange("p t (c i) -> p c t i", i=RUN)

        def quantise(codes, scale_bytes, values):
            nc.vector.quantize_mx(out=codes.bitcast(FP8X4), scales=scale_bytes, in_=values)

        def multiply(result, left_codes, left_bytes, right_codes, right_bytes):
            nc.tensor.matmul_mx(
                out=result,
                lhsT=left_codes.bitcast(FP8X4),
                lhsT_scale=left_bytes,
                rhs=right_codes.bitcast(FP8X4),
                rhs_scale=right_bytes,
                start=True,
                stop=True,
            )

        tab_plane = shared.tile([P, T], U8, name="tab_plane", offset=TAB_PLANE_AT)
        nc.vector.memset(tab_plane[:].bitcast(I32), 0)
        neg_cap = shared.tile([P, 1], F32, name="neg_cap", offset=TAB_AT)
        nc.vector.memset(neg_cap[:], -CAP)
        placed = sb.tile([P, T], F32, name="placed")
        nc.vector.memset(placed[:], 0.0)
        key_plane = shared.tile([P, T], U8, name="key_plane", offset=KEY_PLANE_AT)
        nc.vector.memset(key_plane[:].bitcast(I32), 0)
        tiny = sb.tile([P, 1], F32, name="tiny")
        nc.scalar.activation(tiny[:], neg_cap[:], ACT.Sigmoid)

        w1_raw = shared.tile([P, PACK, HIDDEN], F32, name="w1_raw", offset=W1_AT)
        nc.sync.dma_start(out=w1_raw[:], in_=w1.rearrange("(p t) r -> p t r", t=PACK))
        idx = lists.tile([P, SLOTS // 16], U16, name="idx")
        nc.sync.dma_start(idx[:], offs)
        load_scale_rows(tab_plane, tab_scales)
        tab_pool = shared.tile([P, T], U32, name="tab_pool", offset=TAB_AT)
        load_words(tab_pool, tab_words)
        link = lists.tile([P, SLOTS // 16], U16, name="link")
        nc.sync.dma_start(link[:], offs3)
        load_scale_rows(key_plane, keys_scales)

        tab_bytes = sb.tile([P, SLOTS], U8, name="tab_bytes", align_bytes=64)
        nc.vector.tensor_copy(tab_bytes[:], tab_plane[:].indirect(idx[:]))
        key_pool = shared.tile([P, T], U32, name="key_pool", offset=KEY_AT)
        load_words(key_pool, keys_words)
        w1_bf = sb.tile([P, PACK, P, PACK], BF16, name="w1_bf", align_bytes=64)
        w1_dst = w1_bf[:].rearrange("p j m t -> p m t j")
        w1_src = w1_raw[:].rearrange("p t (m j) -> p m t j", j=PACK)
        nc.scalar.copy(w1_dst[:, :W1_SPLIT], w1_src[:, :W1_SPLIT])
        nc.vector.tensor_copy(w1_dst[:, W1_SPLIT:], w1_src[:, W1_SPLIT:])
        w1_codes = shared.tile([P, HIDDEN], U32, name="w1_codes", offset=W1_CODES_AT, align_bytes=64)
        w1_bytes = sb.tile([P, HIDDEN], U8, name="w1_bytes", align_bytes=64)
        quantise(w1_codes[:], w1_bytes[:], w1_bf[:].rearrange("p j m t -> p (j m t)"))
        tab_codes = sb.tile([P, SLOTS], U32, name="tab_codes", align_bytes=64)
        for h in range(2):
            nc.vector.tensor_copy(tab_codes[:, half(h)], tab_pool[:].indirect(idx[:, half_list(h)]))

        q_raw = shared.tile([P, PACK, P], F32, name="q_raw", offset=W1_AT)
        nc.sync.dma_start(out=q_raw[:], in_=query.rearrange("(p t) q -> p t q", t=PACK))
        g_raw = shared.tile([P, PACK, P], F32, name="g_raw", offset=W1_AT + 4 * PACK * P)
        nc.sync.dma_start(out=g_raw[:], in_=gout.rearrange("(p t) q -> p t q", t=PACK))
        lam_sb = shared.tile([P, PACK], F32, name="lam_sb", offset=VECTORS_AT)
        nc.sync.dma_start(out=lam_sb[:], in_=lam.rearrange("(p j) o -> p (j o)", j=PACK))
        hsc_sb = shared.tile([P, PACK], F32, name="hsc_sb", offset=VECTORS_AT + VECTOR_PITCH)
        nc.sync.dma_start(out=hsc_sb[:], in_=hsc.rearrange("(p j) o -> p (j o)", j=PACK))
        th_sb = shared.tile([P, 1], F32, name="th_sb", offset=VECTORS_AT + 2 * VECTOR_PITCH)
        nc.sync.dma_start(out=th_sb[:], in_=th)
        reserve_sb = shared.tile([P, 1], F32, name="reserve_sb", offset=VECTORS_AT + 3 * VECTOR_PITCH)
        nc.sync.dma_start(out=reserve_sb[:], in_=reserve)

        parts = [(g, h) for h in range(2) for g in range(2)]
        zh = {part: ps.tile([P, 2, HALF], F32, name=f"zh{part[0]}{part[1]}") for part in parts}
        sig_neg = {part: sb.tile([P, 2, HALF], F32, name=f"sig_neg{part[0]}{part[1]}") for part in parts}
        for g, h in parts:
            for e in range(2):
                features = slice((2 * g + e) * P, (2 * g + e + 1) * P)
                multiply(
                    zh[g, h][:, e, :],
                    w1_codes[:, features],
                    w1_bytes[:, features],
                    tab_codes[:, half(h)],
                    tab_bytes[:, half(h)],
                )
            nc.scalar.activation(sig_neg[g, h][:], zh[g, h][:], ACT.Sigmoid, scale=-1.0)

        q_bf = shared.tile([P, P, PACK], BF16, name="q_bf", offset=Q_AT, align_bytes=64)
        key_bytes = shared.tile([P, SLOTS], U8, name="key_bytes", offset=TAB_AT, align_bytes=64)
        nc.vector.tensor_copy(key_bytes[:], key_plane[:].indirect(idx[:]))
        key_codes = sb.tile([P, SLOTS], U32, name="key_codes", align_bytes=64)
        nc.vector.tensor_copy(key_codes[:], key_pool[:].indirect(idx[:]))
        nc.vector.tensor_scalar(woven(q_bf[:]), rows(q_raw[:]), -1.0, None, ALU.mult)
        g_bf = shared.tile([P, P, PACK], BF16, name="g_bf", offset=G_AT, align_bytes=64)
        nc.vector.tensor_copy(woven(g_bf[:]), rows(g_raw[:]))
        q_codes = sb.tile([P, P], U32, name="q_codes", align_bytes=64)
        q_bytes = sb.tile([P, P], U8, name="q_bytes", align_bytes=64)
        quantise(q_codes[:], q_bytes[:], q_bf[:].rearrange("p q t -> p (q t)"))
        neg_a = ps.tile([P, SLOTS], F32, name="neg_a")
        multiply(neg_a[:], q_codes[:], q_bytes[:], key_codes[:], key_bytes[:])

        neg_th = sb.tile([P, 1], F32, name="neg_th")
        nc.gpsimd.tensor_scalar(neg_th[:], th_sb[:], -1.0, 0.0, ALU.mult, ALU.add)
        lam_hsc = sb.tile([P, PACK], F32, name="lam_hsc")
        nc.gpsimd.tensor_tensor(lam_hsc[:], lam_sb[:], hsc_sb[:], ALU.mult)
        old_sb = shared.tile([P, T], F32, name="old_sb", offset=W1_AT)
        nc.sync.dma_start(out=old_sb[:], in_=old)
        g_codes = sb.tile([P, P], U32, name="g_codes", align_bytes=64)
        g_bytes = sb.tile([P, P], U8, name="g_bytes", align_bytes=64)
        quantise(g_codes[:], g_bytes[:], g_bf[:].rearrange("p q t -> p (q t)"))

        log_sig = {part: sb.tile([P, 2, HALF], F32, name=f"log_sig{part[0]}{part[1]}") for part in parts}
        ht = shared.tile([P, HT_COLS], F32, name="ht", offset=HT_AT)
        nc.vector.memset(ht[:, PACK * SLOTS :], 0.0)
        ht_planes = ht[:, : PACK * SLOTS].rearrange("p (j i) -> p j i", j=PACK)
        first_pair = [(0, 0, 0, 1), (0, 0, 1, 2), (0, 1, 0, 2)]
        second_pair = [(1, 0, 0, 2), (1, 1, 0, 2)]
        for g, h, lo, hi in first_pair + second_pair:
            nc.scalar.activation(log_sig[g, h][:, lo:hi, :], sig_neg[g, h][:, lo:hi, :], ACT.Ln, bias=tiny[:])

        linked = [sb.tile([P, SLOTS], F32, name=f"linked{j}") for j in range(PACK)]
        own = [sb.tile([P, SLOTS], F32, name=f"own{j}") for j in range(PACK)]
        hs_planes = sb.tile([P, PACK, SLOTS], BF16, name="hs_planes")

        def finish_softplus(g, h, lo, hi):
            nc.vector.scalar_tensor_tensor(
                ht_planes[:, 2 * g + lo : 2 * g + hi, half(h)],
                log_sig[g, h][:, lo:hi, :],
                -1.0,
                zh[g, h][:, lo:hi, :],
                ALU.mult,
                ALU.max,
            )

        def look_up(j):
            nc.vector.tensor_copy(linked[j][:], ht[:, j * SLOTS : (j + 1) * SLOTS + SPARE].indirect(link[:]))

        def combine(j, slots):
            nc.vector.scalar_tensor_tensor(
                hs_planes[:, j, slots], linked[j][:, slots], lam_hsc[:, j : j + 1], own[j][:, slots], ALU.mult, ALU.add
            )

        for piece in first_pair:
            finish_softplus(*piece)
        look_up(0)
        for piece in second_pair:
            finish_softplus(*piece)
        for j in range(1, PACK):
            look_up(j)

        for h in range(2):
            for j in range(2):
                nc.gpsimd.tensor_scalar(
                    own[j][:, half(h)], ht_planes[:, j, half(h)], hsc_sb[:, j : j + 1], 0.0, ALU.mult, ALU.add
                )
        scaled = sb.tile([P, SLOTS], F32, name="scaled")
        nc.gpsimd.tensor_scalar(scaled[:], linked[0][:], lam_hsc[:, 0:1], 0.0, ALU.mult, ALU.add)
        nc.gpsimd.tensor_tensor(hs_planes[:, 0, :], scaled[:], own[0][:], ALU.add)
        for j in range(2, PACK):
            nc.scalar.activation(own[j][:], ht_planes[:, j, :], ACT.Copy, scale=hsc_sb[:, j : j + 1])

        sig_neg_a = sb.tile([P, SLOTS], F32, name="sig_neg_a", tag="late1", align_bytes=64)
        nc.scalar.activation(sig_neg_a[:], neg_a[:], ACT.Sigmoid, bias=th_sb[:])
        sig_a = sb.tile([P, SLOTS], F32, name="sig_a")
        nc.scalar.activation(sig_a[:], neg_a[:], ACT.Sigmoid, bias=neg_th[:], scale=-1.0)
        log_sig_a = sb.tile([P, SLOTS], F32, name="log_sig_a", tag="late0", align_bytes=64)
        nc.scalar.activation(log_sig_a[:], sig_neg_a[:], ACT.Ln, bias=tiny[:])

        for j in range(1, PACK - 1):
            combine(j, slice(0, SLOTS))
        for h in range(2):
            combine(PACK - 1, half(h))

        hs_bf = [
            sb.tile([P, HALF, PACK], BF16, name="hs_bf0", align_bytes=64),
            sb.tile([P, HALF, PACK], BF16, name="hs_bf1", tag="late1", align_bytes=64),
        ]
        nc.vector.tensor_copy(woven(hs_bf[0][:]), rows(hs_planes[:, :, half(0)]))
        nc.scalar.copy(woven(hs_bf[1][:]), rows(hs_planes[:, :, half(1)]))

        neg_p = sb.tile([P, SLOTS], F32, name="neg_p")
        neg_sum = sb.tile([P, 1], F32, name="neg_sum")
        nc.vector.scalar_tensor_tensor(
            neg_p[:], neg_a[:], th_sb[:], log_sig_a[:], ALU.add, ALU.min, accum_out=neg_sum[:]
        )

        hs_codes = sb.tile([P, SLOTS], U32, name="hs_codes", tag="late0", align_bytes=64)
        hs_bytes = sb.tile([P, SLOTS], U8, name="hs_bytes", align_bytes=64)
        c0 = [ps.tile([P, HALF], F32, name=f"c0_{h}") for h in range(2)]

        def quantise_and_multiply(h):
            quantise(hs_codes[:, half(h)], hs_bytes[:, half(h)], hs_bf[h][:].rearrange("p i t -> p (i t)"))
            multiply(c0[h][:], g_codes[:], g_bytes[:], hs_codes[:, half(h)], hs_bytes[:, half(h)])

        quantise_and_multiply(0)
        z = sb.tile([P, 1], F32, name="z")
        nc.vector.tensor_scalar(z[:], neg_sum[:], -1.0, reserve_sb[:], ALU.mult, ALU.add)
        quantise_and_multiply(1)
        inv_z = sb.tile([P, 1], F32, name="inv_z")
        nc.vector.reciprocal(inv_z[:], z[:])
        gain = sb.tile([P, 1], F32, name="gain")
        nc.vector.tensor_scalar(gain[:], inv_z[:], GRAD_SCALE, None, ALU.mult)
        slope = sb.tile([P, SLOTS], F32, name="slope")
        nc.scalar.activation(slope[:], sig_a[:], ACT.Copy, scale=gain[:])

        terms = sb.tile([P, SLOTS], F32, name="terms")
        shift = [sb.tile([P, 1], F32, name=f"shift{h}") for h in range(2)]
        for h in range(2):
            nc.vector.scalar_tensor_tensor(
                terms[:, half(h)], c0[h][:], inv_z[:], neg_p[:, half(h)], ALU.mult, ALU.mult, accum_out=shift[h][:]
            )
        centred = sb.tile([P, SLOTS], F32, name="centred")
        for h in range(2):
            nc.vector.tensor_scalar(centred[:, half(h)], c0[h][:], shift[0][:], shift[1][:], ALU.add, ALU.add)
        nc.vector.tensor_tensor(placed[:].indirect(idx[:]), centred[:], slope[:], ALU.mult)

        for n in range(T // OUT_CHUNK):
            tokens = slice(n * OUT_CHUNK, (n + 1) * OUT_CHUNK)
            total = sb.tile([P, OUT_CHUNK], F32, name=f"total{n}")
            nc.vector.tensor_tensor(total[:], placed[:, tokens], old_sb[:, tokens], ALU.add)
            queue = nc.sync if n % 2 == 0 else nc.scalar
            queue.dma_start(out=out[:, tokens], in_=total[:])
